import numpy as np, ml_dtypes
CORES = [66,74,82,90,194,202,210,218]
N = 8
import mx_ref
BF = ml_dtypes.bfloat16
def gcols(t, e):
    v = np.concatenate([t.reshape(8, 16, -1, 4), np.zeros((8, 16, 1, 4), BF)], axis=2)
    return np.ascontiguousarray(np.stack([v[g][:, e[g]] for g in range(8)])).reshape(128, -1)
def tile(rs):
    return np.stack(rs, axis=2).reshape(128, -1).astype(BF)
def pick(q, e):
    c = np.concatenate([q[0].reshape(128, -1, 4), np.zeros((128, 1, 4), np.uint8)], axis=1); s = np.concatenate([q[1], np.ones((16, 1), np.uint8)], axis=1)
    return (np.ascontiguousarray(c[:, e].reshape(128, -1)), np.ascontiguousarray(s[:, e]))
def join(*qs):
    return (np.concatenate([q[0] for q in qs], axis=1), np.concatenate([q[1] for q in qs], axis=1))
def put(q, e, v):
    c, s = q[0].reshape(128, -1, 4).copy(), q[1].copy(); c[:, e] = v[0].reshape(128, -1, 4); s[:, e] = v[1]
    return (c.reshape(128, -1), s)
def pk(c, s):
    return (np.ascontiguousarray(c), mx_ref.live(s))
def emit(q):
    return q[0], q[1]
def packed(v, rng):
    q = [mx_ref.quantize(np.ascontiguousarray(v[r])) for r in range(N)]
    return np.stack([a for a, b in q]), np.stack([mx_ref.plane(b, rng) for a, b in q])
def values_of_codes():
    e, c = np.zeros((128, 128, 4), np.float32), np.zeros((128, 2, 4), np.uint8)
    e[np.arange(128), np.arange(128), 0] = 1
    c[:127, :, 0] = np.arange(256).reshape(2, 128).T[:127]
    return mx_ref.matmul(mx_ref.quantize(e.reshape(128, 512).astype(BF)), (c.reshape(128, 8), np.full((16, 2), 127, np.uint8))).T.reshape(-1).astype(np.float64)
CODE_VALUE, SCALE_VALUE = values_of_codes(), 2.0 ** (np.arange(256) - 127.0)
def decode(q):
    return (CODE_VALUE[q[0]].reshape(16, 8, -1, 4) * SCALE_VALUE[q[1]][:, None, :, None] + 0.0).reshape(128, -1).astype(np.float32)
def f(rng, *shape):
    return mx_ref.flush((rng.standard_normal(shape, dtype=np.float32) * np.exp2(rng.integers(-2, 3, shape[:-1] + (1,)))).astype(BF))
def wide(rng, *shape, cols=0):
    v = rng.standard_normal(shape, dtype=np.float32) * np.exp2(rng.integers(-12, 13, shape)).astype(np.float32)
    if cols: v *= np.repeat(np.exp2(rng.integers(-cols, cols + 1, shape[:-2] + (1, shape[-1] // 4))) * (rng.random(shape[:-2] + (1, shape[-1] // 4)) > 0.0625), 4, axis=-1).astype(np.float32)
    return mx_ref.flush(v.astype(BF))
C, K, R, TEAM = 256, 96, 3, 4
def big(v):
    v = v.astype(np.float32)
    v[np.abs(v) < np.float32(2.0 ** -16)] = 0
    return v.astype(BF)
def numbers_of(rng):
    return {"x": big(f(rng, N, 128, 4 * C)), "u": np.array(f(rng, N, 128, 512)), "v": np.array(f(rng, N, 128, 512))}
def layers(rng):
    return big(f(rng, N, 128, 2048)).reshape(N, 8, 16, 4, 8, 16, 4)
def weights(rng, w):
    c, p = packed(np.ascontiguousarray(w).reshape(N, 128, 2048), rng)
    return {"wc": c, "ws": p}
def setup_inputs(rng):
    return {**numbers_of(rng), **weights(rng, layers(rng))}
def setup_inputs_ties(rng):
    d = numbers_of(rng)
    e = rng.permutation(N)
    x = d["x"].reshape(N, 8, 16, C, 4)
    k = rng.integers(0, 3, (N, 8, 2, C))
    k[:, :, 1] = np.where(rng.random((N, 8, C)) < 0.5, k[:, :, 0], k[:, :, 1])
    x[:, :, :2] = 0
    x[:, :, :2, :, 0] = k.astype(np.float32).astype(BF)
    u = d["u"].reshape(N, 128, 128, 4)
    u[:, :, ::16] = 0
    u[:, :, 1::16] = 0
    for r in range(N):
        for h in range(0, 128, 16):
            for i in range(2): u[r, h + i, h + i, 0] = 0.0 if r == e[0] else -1.0 if r == e[1] else 1.0
    w = layers(rng)
    w[:, :, :, :, :, :2] = 0
    return {"x": x.reshape(N, 128, 4 * C), "u": u.reshape(N, 128, 512), "v": d["v"], **weights(rng, w)}
def setup_inputs_near(rng):
    d = numbers_of(rng)
    x = d["x"].astype(np.float32).reshape(N, 8, 16, C, 4)
    x[:, :, 0] = 0
    x[:, :, 8:] = 0
    x[:, :, 0, :, 0] = rng.integers(0, 2, (N, 8, C)) * 2.0 - 1.0
    for r in range(N):
        for g in rng.permutation(8)[:4]: x[r, g, 0, rng.integers(C), 0] = 2.0 ** 28 * rng.choice([-1.0, 1.0])
    s = rng.integers(0, 16, (N, 8, 2, C))
    for i in range(2): x[:, :, 8 + 2 * i] = ((s[:, :, i, :, None] >> np.arange(4)) & 1) * np.exp2(np.arange(4) - 26.0)
    x[:, :, 11, :, 0] = 2.0 ** -13
    x[:, :, 12, :, 0] = (rng.integers(0, 2, (N, 8, C)) * 2.0 - 1.0) * 2.0 ** -27
    u = d["u"].reshape(N, 128, 128, 4)
    u[:, :, ::16] = 0
    u[:, :, 1::16] = 0
    o = rng.permutation(N) % 4
    for r in range(N):
        k = (1.0, 2.0 ** -30, 2.0 ** -33, 2.0 ** 20)[o[r]]
        for h in range(0, 128, 16):
            if o[r] != 2:
                u[r, h, h:h + 2, 0] = k
                u[r, h + 11, h:h + 2, 0] = 8 * k
            else:
                u[r, h + 12, h, 0] = 8 * k
                u[r, h + 12, h + 1, 0] = 9 * k
            u[r, h + 8, h] = 8 * k
            u[r, h + 10, h + 1] = 8 * k
    w = layers(rng)
    for i in [0, 8, 9, 10, 11, 12, 13, 14, 15]:
        w[:, :, i] = 0
        w[:, :, :, :, :, i] = 0
    return {"x": x.reshape(N, 128, 4 * C).astype(BF), "u": u.reshape(N, 128, 512), "v": d["v"], **weights(rng, w)}
def setup_inputs_sides(rng):
    d = numbers_of(rng)
    x = d["x"].reshape(N, 8, 16, C, 4)
    h = rng.permutation(8)
    j = int(rng.integers(80, C // 2 - 15))
    a = rng.integers(0, 2, (N, 8, C)) * 2.0 - 1.0
    q = min(128, C // 2 - 30)
    for r in range(N):
        a[r, h[0]] = 1.0
        a[r, h[1]] = -1.0
        a[r, h[2]] = 1.0 if r % 2 == 1 else -1.0
        a[r, h[3]] = -1.0 if r % 2 == 1 else 1.0
        a[r, h[4]] = np.where(np.arange(C) < j, 1.0, -1.0)
        a[r, h[5]] = np.where(np.arange(C) < j, -1.0, 1.0)
        a[r, h[6]] = 1.0 if r % TEAM == 0 else np.where((np.arange(C) + r) % 3 == 0, 1.0, -1.0)
        a[r, h[7], :q] = 1.0
        a[r, h[7], q:q + 16] = np.where((np.arange(16) + r) % TEAM == 0, -1.0, 1.0)
        a[r, h[7], q + 16:2 * q + 24] = -1.0
    x[:, :, 0] = 0
    x[:, :, 0, :, 0] = a.astype(np.float32).astype(BF)
    k = (N, 8, 8, C, 4)
    x[:, :, 8:] = ((2 * rng.integers(0, 8, k) + 1) * np.exp2(-rng.integers(11, 15, k).astype(np.float32)) * (rng.integers(0, 2, k) * 2 - 1)).astype(np.float32).astype(BF)
    x[:, :, 8, :, 0] = 1.96875
    u = d["u"].reshape(N, 128, 128, 4)
    u[:, :, ::16] = 0
    u[:, :, 1::16] = 0
    for i in range(0, 128, 16): u[:, i, i, 0] = 1.0
    w = layers(rng)
    w[:, :, :, :, :, 8:] = 0
    return {"x": x.reshape(N, 128, 4 * C), "u": u.reshape(N, 128, 512), "v": d["v"], **weights(rng, w)}
def setup_inputs_huge(rng):
    d = numbers_of(rng)
    c = rng.integers(0, 2, (N, 1, 1, C, 1)) * 2.0 - 1.0
    x = 1.75 * 2.0 ** 27 * (0.75 + 0.25 * rng.random((N, 8, 16, C, 4))) * c
    a = np.full((8, 16, 8, 2, 4), 2.0 ** 30, np.float32)
    for g in range(8):
        a[(g + 1) % 8, :, g, 0] *= 0.5
        a[g, :, g, 1] *= 0.5
    u = d["u"].reshape(N, 128, 8, 16, 4)
    u[:, :, :, :2] = a.reshape(128, 8, 2, 4).astype(BF)
    w = (layers(rng).astype(np.float32) * np.float32(2.0 ** -8)).astype(BF)
    return {"x": x.astype(np.float32).reshape(N, 128, 4 * C).astype(BF), "u": u.reshape(N, 128, 512), "v": d["v"], **weights(rng, w)}
def setup_inputs_spread(rng):
    d = setup_inputs(rng)
    d["x"] = big(wide(rng, N, 128, 4 * C, cols=6))
    return d
def check_inputs(d):
    b = []
    for k in ("x", "u", "v"):
        a = np.abs(d[k].astype(np.float32))
        if not (np.isfinite(a).all() and ((a == 0) | (a >= 2.0 ** -30) & (a <= 2.0 ** 30)).all()): b.append("a value of " + k)
    none, least, most = [emit(mx_ref.quantize(np.full((128, 16), k, np.float32).astype(BF)))[1][0, 0] for k in (0.0, 2.0 ** -30, 2.0 ** 30)]
    for r in range(N):
        if ((d["wc"][r] == 0x7F) | (d["wc"][r] == 0xFF)).any(): b.append("wc: a code that is no number")
        s = mx_ref.live(d["ws"][r])
        if ((s != none) & ((s < least) | (s > most))).any(): b.append("ws: a scale out of range")
    return b
def reference(x, u, v, wc, ws):
    qu = [mx_ref.quantize(u[r]) for r in range(N)]
    lay = [pk(wc[r], ws[r]) for r in range(N)]
    now = [x[r] for r in range(N)]
    order = np.zeros((N, 8, C), np.int64)
    for t in range(R):
        vote = np.zeros((N, 8, C), np.int64)
        for r in range(N):
            s = mx_ref.matmul(qu[r], mx_ref.quantize(now[r]))
            vote[r] = np.where(s[::16] >= s[1::16], 1, -1)
        for m in range(0, N, TEAM):
            a = vote[m:m + TEAM].transpose(1, 2, 0).reshape(8, C * TEAM)
            standing = np.cumsum(a, axis=1) - a
            leaves = ((standing >= 0) == (a > 0)).reshape(8, C, TEAM).transpose(2, 0, 1)
            order[m:m + TEAM] = np.argsort(np.where(leaves, 2 * C - np.arange(C), np.arange(C)), axis=2, kind="stable")
        came = [decode(mx_ref.quantize(gcols(now[r], order[r][:, C - K:]))).astype(BF) for r in range(N)]
        made = []
        for r in range(N):
            b = np.concatenate([came[r - 1], gcols(now[r], order[r][:, :C - K])], axis=1).astype(np.float32)
            z = (b - np.roll(b, 2 * C, axis=1) * np.float32(0.5)).astype(BF)
            q = mx_ref.quantize(z)
            made.append(tile([mx_ref.matmul(pick(lay[r], np.arange(128 * i, 128 * i + 128)), q) * np.float32(0.03125) + z[:, i::4].astype(np.float32) for i in range(4)]))
        now = made
    y, od = np.zeros((N, 128, C), np.float32), np.zeros((N, 8, C), np.float32)
    oc, osc = np.zeros((N, 128, 4 * C), np.uint8), np.zeros((N, 16, C), np.uint8)
    for r in range(N):
        q = mx_ref.quantize(now[r])
        y[r] = mx_ref.matmul(mx_ref.quantize(v[r]), q)
        od[r] = order[r]
        oc[r], osc[r] = emit(q)
    return {"y": y, "od": od, "oc": oc, "osc": osc}

@@ -1,0 +1,404 @@
+from concourse.bass import DstId, RemoteDMATransfer
+from concourse.mybir import dt, AluOpType, ActivationFunctionType
+
+C, K, R, TEAM = 256, 96, 3, 4
+H = C // 2
+FP8, U8, BF, F32, I32, U16 = "float8_e4m3fn_x4", "uint8", "bfloat16", "float32", "int32", "uint16"
+
+
+def _s(n, d):
+    return ("sbuf", [128, n], d)
+
+
+SCRATCH = {
+    "X": _s(1024, BF), "X32": _s(1024, BF), "Z": _s(1024, BF), "Z32": _s(1024, BF), "HB": _s(1024, BF), "D": _s(1024, BF),
+    "U": _s(512, BF), "Vv": _s(512, BF), "uq": _s(128, FP8), "us": _s(128, U8), "up": _s(256, FP8), "ups": _s(256, U8),
+    "vq": _s(128, FP8), "vs": _s(128, U8), "wq": _s(512, FP8), "wp": _s(512, U8), "zq": _s(256, FP8), "zs": _s(256, U8),
+    "ET": _s(520, BF), "eq": _s(512, FP8), "es": _s(512, U8),
+    "pi": _s(8, I32), "uo": _s(16, I32), "uo16": _s(16, U16), "IO": _s(256, BF), "I4": _s(160, BF), "PP": _s(16, F32),
+    "TMP": _s(64, F32), "TM4": _s(320, BF),
+    "CD16": _s(128, BF), "CD4": _s(160, BF), "THR": _s(32, F32), "MG": _s(32, F32), "KAP": _s(32, F32), "CK": _s(48, F32),
+    "SBs": _s(256, F32), "AI": _s(512, BF), "DG": _s(512, BF), "THP": _s(32, F32),
+    "S1": _s(48, F32), "S2": _s(32, F32), "GE": _s(32, F32), "TI": _s(64, F32), "TO": _s(64, F32), "LO": _s(96, F32),
+    "T1": _s(32, F32), "T2": _s(32, F32), "PW": _s(32, F32), "PO": _s(32, U16),
+    "NO": _s(256, BF), "NP": _s(256, BF), "DO": _s(160, BF), "DP": _s(96, BF), "OFO": _s(40, U16), "OFP": _s(24, U16),
+    "YS": _s(256, F32),
+    "ps": ("psum", [128, 4096], F32),
+}
+for _r in range(R + 1):
+    SCRATCH["qx%d" % _r] = _s(256, FP8)
+    SCRATCH["sx%d" % _r] = _s(256, U8)
+for _r in range(R):
+    SCRATCH["lc%d" % _r] = _s(256, FP8)
+    SCRATCH["lp%d" % _r] = _s(256, U8)
+    SCRATCH["sb%d" % _r] = _s(48, BF)
+    SCRATCH["ld%d" % _r] = _s(240, BF)
+POOL = {"v": 56, "s": 24, "t": 16, "g": 4, "d": 16, "w": 4}
+SEMAPHORES = ["%s%d" % (q, i) for q in POOL for i in range(POOL[q])] + ["sent"]
+SEMAPHORES += ["%s%d" % (n, r) for n in ("va", "qa", "qb") for r in range(R)]
+
+A = AluOpType
+COPY = ActivationFunctionType.Copy
+
+
+def rank_program(g, core, T, topo):
+    rank = T.rank_of(core)
+    if rank is None:
+        return
+    N = len(T.cores)
+    m, team = rank % TEAM, rank // TEAM
+    eng = {"v": g.vector, "s": g.scalar, "t": g.tensor, "g": g, "y": g.sync}
+    know = {q: set() for q in eng}
+    toks, log, last, waited, turn = [], {}, {}, {}, {q: 0 for q in POOL}
+
+    def cols(v):
+        w = SCRATCH[v[0]][1][1]
+        r = range(*v[1].indices(w))
+        if SCRATCH[v[0]][0] == "psum":
+            return set(c // 512 for c in (r[0], r[-1]))
+        return set(r)
+
+    def B(name, a=None, b=None, s=None):
+        return (name, slice(a, b, s))
+
+    def bank(i):
+        return B("ps", 512 * i, 512 * i + H)
+
+    def ap(v):
+        return T[v[0]][:, v[1]]
+
+    def wait(q, t):
+        if t in know[q]:
+            return
+        sem, val, kn, _ = toks[t]
+        eng[q].wait_ge(T.sem[sem], val)
+        waited[sem] = max(waited.get(sem, 0), val)
+        know[q] |= kn
+        know[q].add(t)
+
+    def order(q, reads, writes):
+        need = set()
+        for v, wr in [(v, False) for v in reads] + [(v, True) for v in writes]:
+            cs = cols(v)
+            ps = SCRATCH[v[0]][0] == "psum"
+            for t, c2, w2 in log.get(v[0], []):
+                if (wr or w2 or (ps and toks[t][3] != q)) and cs & c2:
+                    need.add(t)
+        for t in sorted(need, reverse=True):
+            wait(q, t)
+
+    def note(t, reads, writes):
+        for v, wr in [(v, False) for v in reads] + [(v, True) for v in writes]:
+            log.setdefault(v[0], []).append((t, cols(v), wr))
+
+    def op(q, fn, reads, writes, dma=False):
+        order(q, reads, writes)
+        pool = q if not dma else "w" if q == "g" else "d"
+        sem = "%s%d" % (pool, turn[pool] % POOL[pool])
+        turn[pool] += 1
+        val = 0
+        if sem in last:
+            wait(q, last[sem])
+            val = toks[last[sem]][1]
+        inc = 16 if dma else 1
+        fn().then_inc(T.sem[sem], inc)
+        toks.append((sem, val + inc, set(know[q]), q))
+        last[sem] = len(toks) - 1
+        note(len(toks) - 1, reads, writes)
+        return len(toks) - 1
+
+    def arrival(sem, val, writes):
+        toks.append((sem, val, set(), "far"))
+        last[sem] = len(toks) - 1
+        note(len(toks) - 1, [], writes)
+        return len(toks) - 1
+
+    V, S = g.vector, g.scalar
+
+    def tt(o, a, b, alu):
+        return op("v", lambda: V.tensor_tensor(ap(o), ap(a), ap(b), alu), [a, b], [o])
+
+    def ts(o, a, s1, s2, op0, op1=None):
+        rd = [a] + [s for s in (s1, s2) if isinstance(s, tuple)]
+        a1, a2 = [ap(s) if isinstance(s, tuple) else s for s in (s1, s2)]
+        if op1 is None:
+            return op("v", lambda: V.tensor_scalar(ap(o), ap(a), a1, None, op0), rd, [o])
+        return op("v", lambda: V.tensor_scalar(ap(o), ap(a), a1, a2, op0, op1), rd, [o])
+
+    def cp(o, a):
+        return op("v", lambda: V.tensor_copy(ap(o), ap(a)), [a], [o])
+
+    def fill(o, c):
+        return op("v", lambda: V.memset(ap(o), c), [], [o])
+
+    def scan(o, d0, d1, init, op0, op1):
+        rd = [d0, d1] + ([init] if isinstance(init, tuple) else [])
+        i = ap(init) if isinstance(init, tuple) else init
+        return op("v", lambda: V.tensor_tensor_scan(ap(o), ap(d0), ap(d1), i, op0, op1), rd, [o])
+
+    def tr(o, a):
+        return op("v", lambda: V.transpose(ap(o), ap(a)), [a], [o])
+
+    def quant(c, s, a):
+        return op("v", lambda: V.quantize_mx(ap(c), ap(s), ap(a)), [a], [c, s])
+
+    def act(o, a, scale=1.0):
+        return op("s", lambda: S.activation(ap(o), ap(a), COPY, scale=scale), [a], [o])
+
+    def mm(o, lc, ls, rc, rs):
+        return op("t", lambda: g.tensor.matmul_mx(ap(o), ap(lc), ap(ls), ap(rc), ap(rs), True, True), [lc, ls, rc, rs], [o])
+
+    def dma(q, o, i, reads, writes):
+        return op(q, lambda: eng[q].dma_start(o, i), reads, writes, True)
+
+    def half(name, h, k=1):
+        return B(name, k * H * h, k * H * (h + 1))
+
+    def piece(name, b):
+        return B(name, 128 * b, 128 * b + 128)
+
+    def bits(engines):
+        return sum(1 << e for e in engines)
+
+    sent = [0]
+    nxt = T.cores[(rank + 1) % N]
+
+    def ship(src, dst, sem, codes):
+        order("g", [src], [])
+        rid, pid = topo.addr(nxt, core)
+        a, b = (ap(src).bitcast(dt.uint8), ap(dst).bitcast(dt.uint8)) if codes else (ap(src), ap(dst))
+        g.remote_dma(b, a, T.sem[sem], T.sem.sent, pid, rid, topo.mask(core, nxt))
+        sent[0] += len(topo.engines(core, nxt))
+
+    def slot(k, j):
+        if j == 0:
+            return 64 * (k - 1) + 32
+        if k == j - 1:
+            return 16
+        return 48 + 32 * [i for i in range(TEAM) if i not in (j, j - 1)].index(k)
+
+    def votes(r):
+        sb, ld = "sb%d" % r, "ld%d" % r
+        order("g", [B(sb)], [])
+        plan = []
+        for j in range(TEAM):
+            if j != m:
+                plan.append((team * TEAM + j, 0 if j < m else 16, slot(m, j), 32))
+        far = ((team + 1) * TEAM) % N
+        narrow = r == 0 and m == 1
+        if narrow:
+            plan.append((far, 32, 64 * m + 16, 16))
+        else:
+            plan.append((far, 16, 64 * m, 32) if m < TEAM - 1 else (far, 0, 192, 32))
+        trs = []
+        for i, (d, a, b, w) in enumerate(plan):
+            rid, pid = topo.addr(T.cores[d], core)
+            es = topo.engines(core, T.cores[d])
+            n = len(es) // TEAM
+            trs.append(RemoteDMATransfer(dst_ids=[DstId(rid=rid, pnc=pid)], dma_engine_mask=bits(es[n * i:n * i + n]),
+                                         remote_sem=T.sem["va%d" % r], src=ap(B(sb, a, a + w)), dst=ap(B(ld, b, b + w))))
+            sent[0] += n
+        for part in ([trs[:-1], trs[-1:]] if narrow else [trs]):
+            g.remote_dma_fused(part, local_sem=T.sem.sent)
+
+    def inflow(src, share):
+        return len(topo.engines(T.cores[src], core)) // share
+
+    wo, wp = (16, 0) if m == 0 else (0, 16)
+    q_, q1, plus2, qadd, init, u_, u1, oadd, p_ = [B("PP", i, i + 1) for i in range(9)]
+
+    dma("y", T.X[:, 0:512], T.x[:, 0:512], [], [half("X", 0, 4)])
+    dma("s", T.U[:], T.u[:], [], [B("U")])
+    dma("y", T.X[:, 512:1024], T.x[:, 512:1024], [], [half("X", 1, 4)])
+    op("g", lambda: g.iota(ap(B("pi", 0, 1)), [[0, 1]], 0, 1), [], [B("pi", 0, 1)])
+    op("g", lambda: g.iota(T.uo[:], [[1, 2], [16, 8]], 0, 0), [], [B("uo")])
+    op("g", lambda: g.iota(T.IO[:], [[1, 256]], 0, 0, allow_small_or_imprecise_dtypes=True), [], [B("IO")])
+    op("g", lambda: g.iota(T.I4[:], [[0, 40], [1, 4]], 0, 0, allow_small_or_imprecise_dtypes=True), [], [B("I4")])
+    fill(B("ET"), 0.0)
+    fill(B("MG"), 1.0)
+    fill(B("CK"), 1.0)
+    fill(B("TI", 0, 1), 0.0)
+    ts(B("pi", 1, 2), B("pi", 0, 1), 15, None, A.bitwise_and)
+    ts(B("pi", 3, 4), B("pi", 0, 1), 3, None, A.bitwise_and)
+    cp(p_, B("pi", 0, 1))
+    fill(B("MG", 15, 16), 0.0)
+    fill(B("CK", 16, 17), 4096.0)
+    fill(B("CK", 32, 33), 1.0 / 4096)
+    cp(q_, B("pi", 1, 2))
+    ts(B("pi", 2, 3), B("pi", 1, 2), 2, None, A.arith_shift_right)
+    cp(B("uo16"), B("uo"))
+    ts(q1, q_, 1.0, None, A.add)
+    ts(plus2, q_, 15.0, 2.0, A.is_lt, A.mult)
+    cp(u_, B("pi", 2, 3))
+    cp(B("PP", 9, 10), B("pi", 3, 4))
+    ts(B("TMP", 0, 16), B("IO", 0, 16), q_, 1024.0, A.is_equal, A.mult)
+    ts(B("TMP", 16, 32), B("IO", 0, 16), q1, -2.0, A.is_equal, A.mult)
+    tt(B("CD16", 0, 16), B("TMP", 0, 16), B("TMP", 16, 32), A.add)
+    for n in (16, 32, 64):
+        act(B("CD16", n, 2 * n), B("CD16", 0, n))
+
+    def deciding_columns():
+        quant(B("uq"), B("us"), B("U"))
+        op("s", lambda: S.activation(T.ups[:], T.us[:].indirect(T.uo16[:]), COPY), [B("us"), B("uo16")], [B("ups")])
+        op("v", lambda: V.tensor_copy(T.up[:].bitcast(dt.uint32), T.uq[:].bitcast(dt.uint32).indirect(T.uo16[:])),
+           [B("uq"), B("uo16")], [B("up")])
+
+    def later_constants():
+        ts(B("ET", 3, 515, 4), B("IO", 0, 128), p_, None, A.is_equal)
+        ts(qadd, q_, 0.25, None, A.add)
+        ts(init, q_, -16.0, None, A.mult)
+        ts(u1, u_, 1.0, None, A.add)
+        ts(B("PP", 10, 11), u_, 3.0, 1024.0, A.is_lt, A.mult)
+        ts(B("TMP", 32, 48), B("IO", 0, 16), -1.0, 256.0, A.mult, A.add)
+        ts(B("TMP", 48, 64), B("IO", 0, 16), 16.0, q_, A.mult, A.add)
+        for b in range(4):
+            quant(piece("eq", b), piece("es", b), B("ET", 3 - b, 515 - b))
+        ts(B("TM4", 0, 160), B("I4"), u_, 1024.0, A.is_equal, A.mult)
+        ts(B("TM4", 160, 320), B("I4"), u1, -256.0, A.is_equal, A.mult)
+        tt(oadd, B("PP", 9, 10), B("PP", 10, 11), A.add)
+        for h in range(2):
+            ts(B("KAP", 16 * h, 16 * h + 16), B("TMP", 32, 48), init, None, A.add)
+        ts(B("THR", wo, wo + 16), B("TMP", 48, 64), 2.0, m / 2.0, A.mult, A.add)
+        ts(B("THR", wp, wp + 16), B("TMP", 48, 64), 2.0, ((m - 1) % TEAM) / 2.0, A.mult, A.add)
+        tt(B("CD4"), B("TM4", 0, 160), B("TM4", 160, 320), A.add)
+
+    def quantise_state(r):
+        qx, sx = "qx%d" % r, "sx%d" % r
+        for h in range(2):
+            if h == 1 and r > 0:
+                ts(half("X", 1, 4), half("X32", 1, 4), 0.03125, None, A.mult)
+            quant(half(qx, h), half(sx, h), half("X", h, 4))
+            if r < R:
+                if h == 0:
+                    ship(half(qx, 0), half("lc%d" % r, 0), "qa%d" % r, True)
+                else:
+                    ship(B(sx), B("lp%d" % r), "qa%d" % r, False)
+                if r == 0 and h == 0:
+                    deciding_columns()
+                mm(bank(2 * h), piece("up", 1), piece("ups", 1), half(qx, h), half(sx, h))
+                mm(bank(2 * h + 1), piece("up", 0), piece("ups", 0), half(qx, h), half(sx, h))
+            else:
+                mm(bank(h), B("vq"), B("vs"), half(qx, h), half(sx, h))
+                dma("y", T.oc[:, 512 * h:512 * h + 512], ap(half(qx, h)).bitcast(dt.uint8), [half(qx, h)], [])
+
+    for r in range(R):
+        qx, sx, lc, lp, sb, ld = ["%s%d" % (n, r) for n in ("qx", "sx", "lc", "lp", "sb", "ld")]
+        prev = (rank - 1) % N
+        arrival("qa%d" % r, 2 * inflow(prev, 1), [B(lp), half(lc, 0)])
+        arrival("qb%d" % r, inflow(prev, 1), [half(lc, 1)])
+        senders = [team * TEAM + j for j in range(TEAM) if j != m]
+        if m == 0:
+            senders += [(prev // TEAM) * TEAM + j for j in range(TEAM)]
+        came = arrival("va%d" % r, sum(inflow(s, TEAM) for s in senders), [B(ld, 0, 224) if m == 0 else B(ld, 16, 112)])
+        aown = B(ld, 224, 240) if m == 0 else B(ld, 0, 16)
+
+        quantise_state(r)
+        for h in range(2):
+            act(half("SBs", h), bank(2 * h))
+            tt(half("AI", h), bank(2 * h + 1), half("SBs", h), A.is_ge)
+            scan(half("AI", 2 + h), half("AI", h), half("AI", h), B("AI", C + H - 1, C + H) if h else 0.0, A.add, A.max)
+            scan(half("DG", h), B("CD16"), half("AI", h), 0.0, A.add, A.min)
+            scan(half("DG", 2 + h), B("CD16"), half("AI", 2 + h), 0.0, A.add, A.min)
+        ts(B(sb, 16, 48), B("DG", 15, 512, 16), plus2, None, A.add)
+        tt(B(sb, 0, 16), B("DG", C + 15, 512, 16), B("DG", 15, C, 16), A.subtract)
+        votes(r)
+        ship(half(qx, 1), half(lc, 1), "qb%d" % r, True)
+
+        if r == 0:
+            later_constants()
+            wait("y", came)
+            dma("y", T.wq[:].bitcast(dt.uint8), T.wc[:], [], [B("wq")])
+            dma("y", T.wp[:], T.ws[:], [], [B("wp")])
+            dma("y", T.Vv[:], T.v[:], [], [B("Vv")])
+        if r == R - 1:
+            quant(B("vq"), B("vs"), B("Vv"))
+        cp(aown, B(sb, 16, 32))
+        tt(B("THP", wo, wo + 16), B("THR", wo, wo + 16), B(sb, 0, 16), A.subtract)
+        if m == 0:
+            if r == 0:
+                cp(B("THP", wp, wp + 16), B("THR", wp, wp + 16))
+        else:
+            tt(B("THP", wp, wp + 16), B("THR", wp, wp + 16), B(sb, 0, 16), A.subtract)
+        for h in range(2):
+            for b in range(4):
+                mm(bank(4 - 4 * h + b), piece("eq", b), piece("es", b), half(lc, h), half(lp, h))
+            for b in range(4):
+                act(B("D", 512 * h + b, 512 * h + 512, 4), bank(4 - 4 * h + b))
+
+        if m == 0:
+            tt(B("S1", 0, 32), B(ld, 16, 48), B(ld, 80, 112), A.add)
+            tt(B("S1", 32, 48), B(ld, 144, 160), B(ld, 192, 208), A.add)
+            tt(B("S2", 16, 32), B("S1", 16, 32), B(ld, 160, 176), A.add)
+            tt(B("S2", 0, 16), B("S1", 0, 16), B("S1", 32, 48), A.add)
+            pair = B(ld, 208, 240)
+        else:
+            others = [i for i in range(TEAM) if i not in (m, m - 1)]
+            x1, x2 = [slot(k, m) + (16 if k < m else 0) for k in others]
+            tt(B("S1", 0, 16), B(ld, 32, 48), B(ld, x1, x1 + 16), A.add)
+            tt(B("S1", 16, 32), B(ld, x2, x2 + 16), B(ld, 16, 32), A.subtract)
+            tt(B("S2", 0, 16), B("S1", 0, 16), B(ld, x2, x2 + 16), A.add)
+            tt(B("S2", 16, 32), B("S1", 0, 16), B("S1", 16, 32), A.add)
+            pair = B(ld, 0, 32)
+        tt(B("GE"), B("S2"), B("THP"), A.is_ge)
+        tt(B("TI", 32, 64), B("GE"), pair, A.is_equal)
+        scan(B("TI", 1, 32), B("TI", 32, 63), B("MG", 0, 31), 0.0, A.add, A.mult)
+        tr(B("TO"), B("TI"))
+        for h in range(2):
+            scan(B("LO", 48 * h, 48 * h + 48), B("CK"), B("TO", 16 * h, 16 * h + 48), init, A.mult, A.add)
+        tt(B("T1"), B("TO", 32, 64), B("KAP"), A.mult)
+        for h in range(2):
+            tt(B("T2", 16 * h, 16 * h + 16), B("T1", 16 * h, 16 * h + 16), B("LO", 48 * h + 32, 48 * h + 48), A.subtract)
+        tr(B("PW"), B("T2"))
+        ts(B("PO"), B("PW"), qadd, None, A.add)
+
+        def minus_half(a, b, win, off):
+            o = B("HB", 4 * a, 4 * b)
+            op("s", lambda: S.activation(ap(o), T[win][:].indirect(ap(off)), COPY, scale=-0.5), [B(win), off], [o])
+
+        def zpart(a, b, win, off):
+            o, hb = B("Z", 4 * a, 4 * b), B("HB", 4 * ((a + H) % C), 4 * ((a + H) % C + b - a))
+            op("v", lambda: V.tensor_tensor(ap(o), T[win][:].indirect(ap(off)), ap(hb), A.add), [B(win), off, hb], [o])
+
+        for w, nn, a, b, dg, of in ((wo, "NO", 0, C - K, "DO", "OFO"), (wp, "NP", C - K, C, "DP", "OFP")):
+            op("v", lambda: V.tensor_copy(T[nn][:].indirect(ap(B("PO", w, w + 16))), T.IO[:]), [B("IO"), B("PO", w, w + 16)], [B(nn)])
+            if nn == "NP":
+                zpart(K, H, "X", B("OFO", 0, 8))
+            scan(B(dg), B("CD4", 0, b - a), B(nn, a, b), 0.0, A.add, A.min)
+            if nn == "NP":
+                zpart(H + K, C, "X", B("OFO", 32, 40))
+            ts(B(of), B(dg, 3, b - a, 4), 4.0, oadd, A.mult, A.add)
+            if nn == "NO":
+                minus_half(H + K, C, "X", B("OFO", 32, 40))
+                minus_half(K, H, "X", B("OFO", 0, 8))
+                minus_half(H, H + K, "X", B("OFO", 8, 32))
+                if r == R - 1:
+                    dma("g", T.od[:], T.NO[0:128:16, :], [B("NO")], [])
+            else:
+                minus_half(0, K, "D", B("OFP"))
+
+        for h in range(2):
+            if h == 0:
+                zpart(0, K, "D", B("OFP"))
+            else:
+                zpart(H, H + K, "X", B("OFO", 8, 32))
+            quant(half("zq", h), half("zs", h), half("Z", h, 4))
+            act(half("Z32", h, 4), half("Z", h, 4), 32.0)
+            for b in range(4):
+                mm(bank(4 * h + b), piece("wq", b), piece("wp", b), half("zq", h), half("zs", h))
+        for h in range(2):
+            for b in range(4):
+                tt(B("X32", 512 * h + b, 512 * h + 512, 4), bank(4 * h + b), B("Z32", 512 * h + b, 512 * h + 512, 4), A.add)
+            if h == 0:
+                act(half("X", 0, 4), half("X32", 0, 4), 0.03125)
+
+    quantise_state(R)
+    sx = "sx%d" % R
+    for k in range(4):
+        dma("s" if k < 2 else "g", T.osc[4 * k:4 * k + 4, :], T[sx][32 * k:32 * k + 4, :], [B(sx)], [])
+    for h in range(2):
+        cp(half("YS", h), bank(h))
+        dma("y" if h else "s", T.y[:, H * h:H * h + H], ap(half("YS", h)), [half("YS", h)], [])
+    g.wait_ge(T.sem.sent, sent[0])
+    for t in sorted(last.values()):
+        if waited.get(toks[t][0], 0) < toks[t][1]:
+            g.wait_ge(T.sem[toks[t][0]], toks[t][1])

@@ -265,14 +265,10 @@ def rank_program(g, core, T, topo):
     def quantise_state(r):
         qx, sx = "qx%d" % r, "sx%d" % r
         for h in range(2):
-            if h == 1 and r > 0:
-                ts(half("X", 1, 4), half("X32", 1, 4), 0.03125, None, A.mult)
             quant(half(qx, h), half(sx, h), half("X", h, 4))
             if r < R:
                 if h == 0:
                     ship(half(qx, 0), half("lc%d" % r, 0), "qa%d" % r, True)
-                else:
-                    ship(B(sx), B("lp%d" % r), "qa%d" % r, False)
                 if r == 0 and h == 0:
                     deciding_columns()
                 mm(bank(2 * h), piece("up", 1), piece("ups", 1), half(qx, h), half(sx, h))
@@ -293,15 +289,22 @@ def rank_program(g, core, T, topo):
         aown = B(ld, 224, 240) if m == 0 else B(ld, 0, 16)
 
         quantise_state(r)
+
+        def own_column(k):
+            scan(half("DG", k), B("CD16"), half("AI", k), 0.0, A.add, A.min)
+
         for h in range(2):
             act(half("SBs", h), bank(2 * h))
             tt(half("AI", h), bank(2 * h + 1), half("SBs", h), A.is_ge)
+            if h:
+                own_column(2)
             scan(half("AI", 2 + h), half("AI", h), half("AI", h), B("AI", C + H - 1, C + H) if h else 0.0, A.add, A.max)
-            scan(half("DG", h), B("CD16"), half("AI", h), 0.0, A.add, A.min)
-            scan(half("DG", 2 + h), B("CD16"), half("AI", 2 + h), 0.0, A.add, A.min)
+            own_column(h)
+        own_column(3)
         ts(B(sb, 16, 48), B("DG", 15, 512, 16), plus2, None, A.add)
         tt(B(sb, 0, 16), B("DG", C + 15, 512, 16), B("DG", 15, C, 16), A.subtract)
         votes(r)
+        ship(B(sx), B(lp), "qa%d" % r, False)
         ship(half(qx, 1), half(lc, 1), "qb%d" % r, True)
 
         if r == 0:
@@ -309,7 +312,8 @@ def rank_program(g, core, T, topo):
             wait("y", came)
             dma("y", T.wq[:].bitcast(dt.uint8), T.wc[:], [], [B("wq")])
             dma("y", T.wp[:], T.ws[:], [], [B("wp")])
-            dma("y", T.Vv[:], T.v[:], [], [B("Vv")])
+        if r == 1:
+            dma("y", T.Vv[:], T.v[:], [B("X", 0, 4)], [B("Vv")])
         if r == R - 1:
             quant(B("vq"), B("vs"), B("Vv"))
         cp(aown, B(sb, 16, 32))
@@ -376,25 +380,32 @@ def rank_program(g, core, T, topo):
             else:
                 minus_half(0, K, "D", B("OFP"))
 
+        def times32(a, b):
+            act(B("Z32", 4 * a, 4 * b), B("Z", 4 * a, 4 * b), 32.0)
+
         for h in range(2):
             if h == 0:
                 zpart(0, K, "D", B("OFP"))
             else:
                 zpart(H, H + K, "X", B("OFO", 8, 32))
             quant(half("zq", h), half("zs", h), half("Z", h, 4))
-            act(half("Z32", h, 4), half("Z", h, 4), 32.0)
+            if h == 0:
+                times32(0, H)
+                times32(H + K, C)
+            else:
+                times32(H, H + K)
             for b in range(4):
                 mm(bank(4 * h + b), piece("wq", b), piece("wp", b), half("zq", h), half("zs", h))
         for h in range(2):
             for b in range(4):
-                tt(B("X32", 512 * h + b, 512 * h + 512, 4), bank(4 * h + b), B("Z32", 512 * h + b, 512 * h + 512, 4), A.add)
-            if h == 0:
-                act(half("X", 0, 4), half("X32", 0, 4), 0.03125)
+                rows = (512 * h + b, 512 * h + 512, 4)
+                tt(B("X32", *rows), bank(4 * h + b), B("Z32", *rows), A.add)
+                act(B("X", *rows), B("X32", *rows), 0.03125)
 
     quantise_state(R)
     sx = "sx%d" % R
     for k in range(4):
-        dma("s" if k < 2 else "g", T.osc[4 * k:4 * k + 4, :], T[sx][32 * k:32 * k + 4, :], [B(sx)], [])
+        dma("s" if k < 2 else "y", T.osc[4 * k:4 * k + 4, :], T[sx][32 * k:32 * k + 4, :], [B(sx)], [])
     for h in range(2):
         cp(half("YS", h), bank(h))
         dma("y" if h else "s", T.y[:, H * h:H * h + H], ap(half("YS", h)), [half("YS", h)], [])

@@ -15,12 +15,14 @@ SCRATCH = {
     "U": _s(512, BF), "Vv": _s(512, BF), "uq": _s(128, FP8), "us": _s(128, U8), "up": _s(256, FP8), "ups": _s(256, U8),
     "vq": _s(128, FP8), "vs": _s(128, U8), "wq": _s(512, FP8), "wp": _s(512, U8), "zq": _s(256, FP8), "zs": _s(256, U8),
     "ET": _s(520, BF), "eq": _s(512, FP8), "es": _s(512, U8),
-    "pi": _s(8, I32), "uo": _s(16, I32), "uo16": _s(16, U16), "IO": _s(256, BF), "I4": _s(160, BF), "PP": _s(16, F32),
-    "TMP": _s(64, F32), "TM4": _s(320, BF),
-    "CD16": _s(128, BF), "CD4": _s(160, BF), "THR": _s(32, F32), "MG": _s(32, F32), "KAP": _s(32, F32), "CK": _s(48, F32),
-    "SBs": _s(256, F32), "AI": _s(512, BF), "DG": _s(512, BF), "THP": _s(32, F32),
-    "S1": _s(48, F32), "S2": _s(32, F32), "GE": _s(32, F32), "TI": _s(64, F32), "TO": _s(64, F32), "LO": _s(96, F32),
-    "T1": _s(32, F32), "T2": _s(32, F32), "PW": _s(32, F32), "PO": _s(32, U16),
+    "pi": _s(8, I32), "uo": _s(16, I32), "uo16": _s(16, U16), "IO": _s(256, BF), "I4": _s(160, BF), "I16": _s(128, BF),
+    "PP": _s(16, F32), "TMP": _s(16, F32), "TM4": _s(320, BF), "NE": _s(128, BF),
+    "HALF": _s(256, BF), "FROM": _s(128, BF), "PAST": _s(128, BF),
+    "CD4": _s(160, BF), "MG": _s(32, F32), "KAP": _s(32, F32), "CK": _s(48, F32),
+    "SBs": _s(256, F32), "AI": _s(256, BF), "TS": _s(256, BF), "HP": _s(256, BF), "HI": _s(256, BF),
+    "LP": _s(32, BF), "AT": _s(32, BF),
+    "S1": _s(32, F32), "S2": _s(32, F32), "GE": _s(32, F32), "TI": _s(64, F32), "TO": _s(64, F32), "LO": _s(96, F32),
+    "ONE": _s(256, BF), "TK": _s(32, F32), "T1": _s(32, F32), "T2": _s(32, F32), "PW": _s(32, F32), "PO": _s(32, U16),
     "NO": _s(256, BF), "NP": _s(256, BF), "DO": _s(160, BF), "DP": _s(96, BF), "OFO": _s(40, U16), "OFP": _s(24, U16),
     "YS": _s(256, F32),
     "ps": ("psum", [128, 4096], F32),
@@ -33,12 +35,15 @@ for _r in range(R):
     SCRATCH["lp%d" % _r] = _s(256, U8)
     SCRATCH["sb%d" % _r] = _s(48, BF)
     SCRATCH["ld%d" % _r] = _s(240, BF)
-POOL = {"v": 56, "s": 24, "t": 16, "g": 4, "d": 16, "w": 4}
-SEMAPHORES = ["%s%d" % (q, i) for q in POOL for i in range(POOL[q])] + ["sent"]
+SHARED = ["k%d" % i for i in range(120)]
+ONCE = ["d%d" % i for i in range(16)]
+SEMAPHORES = SHARED + ONCE + ["sent"]
 SEMAPHORES += ["%s%d" % (n, r) for n in ("va", "qa", "qb") for r in range(R)]
 
 A = AluOpType
 COPY = ActivationFunctionType.Copy
+
+RUNS = ("IIP", "IIP", "IPP", "PPI")
 
 
 def rank_program(g, core, T, topo):
@@ -49,7 +54,7 @@ def rank_program(g, core, T, topo):
     m, team = rank % TEAM, rank // TEAM
     eng = {"v": g.vector, "s": g.scalar, "t": g.tensor, "g": g, "y": g.sync}
     know = {q: set() for q in eng}
-    toks, log, last, waited, turn = [], {}, {}, {}, {q: 0 for q in POOL}
+    calls, log = [], {}
 
     def cols(v):
         w = SCRATCH[v[0]][1][1]
@@ -67,51 +72,78 @@ def rank_program(g, core, T, topo):
     def ap(v):
         return T[v[0]][:, v[1]]
 
-    def wait(q, t):
-        if t in know[q]:
-            return
-        sem, val, kn, _ = toks[t]
-        eng[q].wait_ge(T.sem[sem], val)
-        waited[sem] = max(waited.get(sem, 0), val)
-        know[q] |= kn
-        know[q].add(t)
-
-    def order(q, reads, writes):
-        need = set()
+    def order(q, reads, writes, more):
+        need = set(more)
         for v, wr in [(v, False) for v in reads] + [(v, True) for v in writes]:
             cs = cols(v)
             ps = SCRATCH[v[0]][0] == "psum"
             for t, c2, w2 in log.get(v[0], []):
-                if (wr or w2 or (ps and toks[t][3] != q)) and cs & c2:
+                if (wr or w2 or (ps and calls[t][0] != q)) and cs & c2:
                     need.add(t)
+        waits = []
         for t in sorted(need, reverse=True):
-            wait(q, t)
+            if t not in know[q]:
+                waits.append(t)
+                know[q] |= calls[t][3] | {t}
+        return waits
 
-    def note(t, reads, writes):
+    def op(q, fn, reads, writes, kind="c", more=()):
+        waits = order(q, reads, writes, more) if q in know else []
+        calls.append((q, fn, waits, set(know.get(q, ())), kind))
         for v, wr in [(v, False) for v in reads] + [(v, True) for v in writes]:
-            log.setdefault(v[0], []).append((t, cols(v), wr))
-
-    def op(q, fn, reads, writes, dma=False):
-        order(q, reads, writes)
-        pool = q if not dma else "w" if q == "g" else "d"
-        sem = "%s%d" % (pool, turn[pool] % POOL[pool])
-        turn[pool] += 1
-        val = 0
-        if sem in last:
-            wait(q, last[sem])
-            val = toks[last[sem]][1]
-        inc = 16 if dma else 1
-        fn().then_inc(T.sem[sem], inc)
-        toks.append((sem, val + inc, set(know[q]), q))
-        last[sem] = len(toks) - 1
-        note(len(toks) - 1, reads, writes)
-        return len(toks) - 1
+            log.setdefault(v[0], []).append((len(calls) - 1, cols(v), wr))
+        return len(calls) - 1
 
     def arrival(sem, val, writes):
-        toks.append((sem, val, set(), "far"))
-        last[sem] = len(toks) - 1
-        note(len(toks) - 1, [], writes)
-        return len(toks) - 1
+        return op("far", (sem, val), [], writes, "far")
+
+    def issue():
+        by = {t: set() for t in range(len(calls))}
+        for c, call in enumerate(calls):
+            for t in call[2]:
+                by[t].add(c)
+        lot = {t: [t] for t in by}
+
+        def free(c, t, both):
+            return t in calls[c][3] or any(u > t and calls[u][0] == calls[t][0] and calls[t][4] == "c" and c in by[u] for u in both)
+
+        for call in calls:
+            for i, t in enumerate(call[2]):
+                for u in call[2][:i]:
+                    both = lot[t] + lot[u]
+                    if lot[t] is not lot[u] and calls[t][4] == calls[u][4] != "far" and all(
+                            free(c, x, both) for y in both for c in by[y] for x in both):
+                        for x in both:
+                            lot[x] = both
+        done, seen = {q: set() for q in eng}, []
+        for c, (q, fn, waits, _, kind) in enumerate(calls):
+            for t in list(waits):
+                if t in done[q]:
+                    waits.remove(t)
+                for x in lot[t]:
+                    done[q] |= seen[x] | {x}
+            seen.append(set(done.get(q, ())))
+        sem_of, held, once = {}, [(n, 0, []) for n in SHARED], list(ONCE)
+        for c, (q, fn, waits, _, kind) in enumerate(calls):
+            mine = lot[c]
+            if kind == "far":
+                sem_of[c] = fn
+                continue
+            if c not in sem_of and any(by[x] for x in mine):
+                if kind == "c":
+                    i = min(i for i, h in enumerate(held) if all(y in seen[x] for y in h[2] for x in mine))
+                    n, val, _ = held.pop(i)
+                    val += len(mine)
+                    held.append((n, val, mine))
+                else:
+                    n, val = once.pop(), 16 * len(mine)
+                for x in mine:
+                    sem_of[x] = (n, val)
+            for t in waits:
+                eng[q].wait_ge(T.sem[sem_of[t][0]], sem_of[t][1])
+            made = fn()
+            if c in sem_of:
+                made.then_inc(T.sem[sem_of[c][0]], 1 if kind == "c" else 16)
 
     V, S = g.vector, g.scalar
 
@@ -148,8 +180,12 @@ def rank_program(g, core, T, topo):
     def mm(o, lc, ls, rc, rs):
         return op("t", lambda: g.tensor.matmul_mx(ap(o), ap(lc), ap(ls), ap(rc), ap(rs), True, True), [lc, ls, rc, rs], [o])
 
-    def dma(q, o, i, reads, writes):
-        return op(q, lambda: eng[q].dma_start(o, i), reads, writes, True)
+    def dma(q, o, i, reads, writes, more=()):
+        return op(q, lambda: eng[q].dma_start(o, i), reads, writes, "soft" if q == "g" else "hard", more)
+
+    def iota(o, pattern, step=0):
+        small = SCRATCH[o[0]][2] != I32
+        return op("g", lambda: g.iota(ap(o), pattern, 0, step, allow_small_or_imprecise_dtypes=small), [], [o])
 
     def half(name, h, k=1):
         return B(name, k * H * h, k * H * (h + 1))
@@ -161,255 +197,270 @@ def rank_program(g, core, T, topo):
         return sum(1 << e for e in engines)
 
     sent = [0]
-    nxt = T.cores[(rank + 1) % N]
+    nxt, prev = T.cores[(rank + 1) % N], (rank - 1) % N
 
     def ship(src, dst, sem, codes):
-        order("g", [src], [])
         rid, pid = topo.addr(nxt, core)
         a, b = (ap(src).bitcast(dt.uint8), ap(dst).bitcast(dt.uint8)) if codes else (ap(src), ap(dst))
-        g.remote_dma(b, a, T.sem[sem], T.sem.sent, pid, rid, topo.mask(core, nxt))
+        op("g", lambda: g.remote_dma(b, a, T.sem[sem], T.sem.sent, pid, rid, topo.mask(core, nxt)), [src], [])
         sent[0] += len(topo.engines(core, nxt))
-
-    def slot(k, j):
-        if j == 0:
-            return 64 * (k - 1) + 32
-        if k == j - 1:
-            return 16
-        return 48 + 32 * [i for i in range(TEAM) if i not in (j, j - 1)].index(k)
 
     def votes(r):
         sb, ld = "sb%d" % r, "ld%d" % r
-        order("g", [B(sb)], [])
         plan = []
         for j in range(TEAM):
             if j != m:
-                plan.append((team * TEAM + j, 0 if j < m else 16, slot(m, j), 32))
-        far = ((team + 1) * TEAM) % N
+                want = "IP" if j == m + 1 else "II" if j > m else "PP" if j else RUNS[m][1:] if m < TEAM - 1 else "PP"
+                plan.append((team * TEAM + j, 16 * RUNS[m].index(want), 32 * m if j else 64 * (m - 1), 32))
         narrow = r == 0 and m == 1
-        if narrow:
-            plan.append((far, 32, 64 * m + 16, 16))
-        else:
-            plan.append((far, 16, 64 * m, 32) if m < TEAM - 1 else (far, 0, 192, 32))
+        plan.append((((team + 1) * TEAM) % N, 16 if m == TEAM - 1 else 0, (32, 96, 208, 160)[m], 16 if narrow else 32))
         trs = []
         for i, (d, a, b, w) in enumerate(plan):
             rid, pid = topo.addr(T.cores[d], core)
             es = topo.engines(core, T.cores[d])
             n = len(es) // TEAM
-            trs.append(RemoteDMATransfer(dst_ids=[DstId(rid=rid, pnc=pid)], dma_engine_mask=bits(es[n * i:n * i + n]),
-                                         remote_sem=T.sem["va%d" % r], src=ap(B(sb, a, a + w)), dst=ap(B(ld, b, b + w))))
+            trs.append((RemoteDMATransfer(dst_ids=[DstId(rid=rid, pnc=pid)], dma_engine_mask=bits(es[n * i:n * i + n]),
+                                          remote_sem=T.sem["va%d" % r], src=ap(B(sb, a, a + w)), dst=ap(B(ld, b, b + w))), B(sb, a, a + w)))
             sent[0] += n
-        for part in ([trs[:-1], trs[-1:]] if narrow else [trs]):
-            g.remote_dma_fused(part, local_sem=T.sem.sent)
+        for part in ([trs[-1:], trs[:-1]] if narrow else [trs]):
+            op("g", lambda part=part: g.remote_dma_fused([t for t, _ in part], local_sem=T.sem.sent), [v for _, v in part], [])
 
     def inflow(src, share):
         return len(topo.engines(T.cores[src], core)) // share
 
-    wo, wp = (16, 0) if m == 0 else (0, 16)
-    q_, q1, plus2, qadd, init, u_, u1, oadd, p_ = [B("PP", i, i + 1) for i in range(9)]
+    p_, q_, u_, t_, low, qadd, init, u1, ufix, oadd = [B("PP", i, i + 1) for i in range(10)]
 
     dma("y", T.X[:, 0:512], T.x[:, 0:512], [], [half("X", 0, 4)])
-    dma("s", T.U[:], T.u[:], [], [B("U")])
+    dma("y", T.U[:], T.u[:], [], [B("U")])
     dma("y", T.X[:, 512:1024], T.x[:, 512:1024], [], [half("X", 1, 4)])
-    op("g", lambda: g.iota(ap(B("pi", 0, 1)), [[0, 1]], 0, 1), [], [B("pi", 0, 1)])
-    op("g", lambda: g.iota(T.uo[:], [[1, 2], [16, 8]], 0, 0), [], [B("uo")])
-    op("g", lambda: g.iota(T.IO[:], [[1, 256]], 0, 0, allow_small_or_imprecise_dtypes=True), [], [B("IO")])
-    op("g", lambda: g.iota(T.I4[:], [[0, 40], [1, 4]], 0, 0, allow_small_or_imprecise_dtypes=True), [], [B("I4")])
+    iota(B("pi", 0, 1), [[0, 1]], 1)
+    iota(B("uo"), [[1, 2], [16, 8]])
+    iota(B("I16"), [[0, 8], [1, 16]])
+    iota(B("I4"), [[0, 40], [1, 4]])
+    fill(B("ONE"), 1.0)
     fill(B("ET"), 0.0)
+    fill(B("HALF"), -0.5)
+    scan(B("IO"), B("ONE"), B("ONE"), -1.0, A.add, A.mult)
+    ts(B("pi", 1, 2), B("pi", 0, 1), 15, None, A.bitwise_and)
+    ts(B("pi", 2, 3), B("pi", 0, 1), 2, 3, A.arith_shift_right, A.bitwise_and)
+    ts(B("pi", 3, 4), B("pi", 0, 1), 3, None, A.bitwise_and)
+    cp(B("uo16"), B("uo"))
     fill(B("MG"), 1.0)
     fill(B("CK"), 1.0)
-    fill(B("TI", 0, 1), 0.0)
-    ts(B("pi", 1, 2), B("pi", 0, 1), 15, None, A.bitwise_and)
-    ts(B("pi", 3, 4), B("pi", 0, 1), 3, None, A.bitwise_and)
-    cp(p_, B("pi", 0, 1))
-    fill(B("MG", 15, 16), 0.0)
-    fill(B("CK", 16, 17), 4096.0)
-    fill(B("CK", 32, 33), 1.0 / 4096)
-    cp(q_, B("pi", 1, 2))
-    ts(B("pi", 2, 3), B("pi", 1, 2), 2, None, A.arith_shift_right)
-    cp(B("uo16"), B("uo"))
-    ts(q1, q_, 1.0, None, A.add)
-    ts(plus2, q_, 15.0, 2.0, A.is_lt, A.mult)
-    cp(u_, B("pi", 2, 3))
-    cp(B("PP", 9, 10), B("pi", 3, 4))
-    ts(B("TMP", 0, 16), B("IO", 0, 16), q_, 1024.0, A.is_equal, A.mult)
-    ts(B("TMP", 16, 32), B("IO", 0, 16), q1, -2.0, A.is_equal, A.mult)
-    tt(B("CD16", 0, 16), B("TMP", 0, 16), B("TMP", 16, 32), A.add)
-    for n in (16, 32, 64):
-        act(B("CD16", n, 2 * n), B("CD16", 0, n))
+    cp(B("PP", 0, 4), B("pi", 0, 4))
 
-    def deciding_columns():
-        quant(B("uq"), B("us"), B("U"))
-        op("s", lambda: S.activation(T.ups[:], T.us[:].indirect(T.uo16[:]), COPY), [B("us"), B("uo16")], [B("ups")])
-        op("v", lambda: V.tensor_copy(T.up[:].bitcast(dt.uint32), T.uq[:].bitcast(dt.uint32).indirect(T.uo16[:])),
-           [B("uq"), B("uo16")], [B("up")])
-
-    def later_constants():
-        ts(B("ET", 3, 515, 4), B("IO", 0, 128), p_, None, A.is_equal)
-        ts(qadd, q_, 0.25, None, A.add)
-        ts(init, q_, -16.0, None, A.mult)
+    def constants_of_the_votes():
+        ts(low, q_, 0.5, -8.0, A.mult, A.add)
+        ts(B("NE"), B("I16"), q_, 1024.0, A.not_equal, A.mult)
         ts(u1, u_, 1.0, None, A.add)
-        ts(B("PP", 10, 11), u_, 3.0, 1024.0, A.is_lt, A.mult)
-        ts(B("TMP", 32, 48), B("IO", 0, 16), -1.0, 256.0, A.mult, A.add)
-        ts(B("TMP", 48, 64), B("IO", 0, 16), 16.0, q_, A.mult, A.add)
-        for b in range(4):
-            quant(piece("eq", b), piece("es", b), B("ET", 3 - b, 515 - b))
+
+    def patterns_of_the_votes():
+        ts(B("FROM"), B("NE"), low, None, A.add)
+        ts(B("PAST"), B("NE"), low, 0.5, A.add, A.add)
+
+    def deciding_columns(k):
+        off = B("uo16", 8 * k, 8 * k + 8)
+        op("s", lambda: S.activation(ap(piece("ups", k)), T.us[:].indirect(ap(off)), COPY), [B("us"), off], [piece("ups", k)])
+        op("v", lambda: V.tensor_copy(ap(piece("up", k)).bitcast(dt.uint32), T.uq[:].bitcast(dt.uint32).indirect(ap(off))),
+           [B("uq"), off], [piece("up", k)])
+
+    def constants_of_the_orders():
+        ts(B("ET", 3, 515, 4), B("IO", 0, 128), p_, None, A.is_equal)
+        ts(ufix, u_, 3.0, 1024.0, A.is_lt, A.mult)
+        ts(B("TMP"), B("IO", 0, 16), -16.0, 256.0, A.mult, A.add)
         ts(B("TM4", 0, 160), B("I4"), u_, 1024.0, A.is_equal, A.mult)
         ts(B("TM4", 160, 320), B("I4"), u1, -256.0, A.is_equal, A.mult)
-        tt(oadd, B("PP", 9, 10), B("PP", 10, 11), A.add)
+
+    def constants_of_the_unpacking():
+        for b in range(4):
+            quant(piece("eq", b), piece("es", b), B("ET", 3 - b, 515 - b))
+        fill(B("TI", 0, 1), 0.0)
+        fill(B("MG", 15, 16), 0.0)
+        fill(B("CK", 16, 17), 4096.0)
+        fill(B("CK", 32, 33), 1.0 / 4096)
+        ts(qadd, q_, 0.25, None, A.add)
+        ts(init, q_, -16.0, None, A.mult)
+        tt(oadd, t_, ufix, A.add)
         for h in range(2):
-            ts(B("KAP", 16 * h, 16 * h + 16), B("TMP", 32, 48), init, None, A.add)
-        ts(B("THR", wo, wo + 16), B("TMP", 48, 64), 2.0, m / 2.0, A.mult, A.add)
-        ts(B("THR", wp, wp + 16), B("TMP", 48, 64), 2.0, ((m - 1) % TEAM) / 2.0, A.mult, A.add)
+            ts(B("KAP", 16 * h, 16 * h + 16), B("TMP"), q_, None, A.subtract)
         tt(B("CD4"), B("TM4", 0, 160), B("TM4", 160, 320), A.add)
 
-    def quantise_state(r):
+    def quantise_state(r, h):
         qx, sx = "qx%d" % r, "sx%d" % r
+        quant(half(qx, h), half(sx, h), half("X", h, 4))
+        if r < R and h == 0:
+            ship(half(qx, 0), half("lc%d" % r, 0), "qa%d" % r, True)
+
+    def score(r, h, k):
+        mm(bank(2 * h + 1 - k), piece("up", k), piece("ups", k), half("qx%d" % r, h), half("sx%d" % r, h))
+
+    quantise_state(0, 0)
+    constants_of_the_votes()
+    quant(B("uq"), B("us"), B("U"))
+    patterns_of_the_votes()
+    deciding_columns(1)
+    quantise_state(0, 1)
+    deciding_columns(0)
+    for k in (1, 0):
         for h in range(2):
-            quant(half(qx, h), half(sx, h), half("X", h, 4))
-            if r < R:
-                if h == 0:
-                    ship(half(qx, 0), half("lc%d" % r, 0), "qa%d" % r, True)
-                if r == 0 and h == 0:
-                    deciding_columns()
-                mm(bank(2 * h), piece("up", 1), piece("ups", 1), half(qx, h), half(sx, h))
-                mm(bank(2 * h + 1), piece("up", 0), piece("ups", 0), half(qx, h), half(sx, h))
-            else:
-                mm(bank(h), B("vq"), B("vs"), half(qx, h), half(sx, h))
-                dma("y", T.oc[:, 512 * h:512 * h + 512], ap(half(qx, h)).bitcast(dt.uint8), [half(qx, h)], [])
+            score(0, h, k)
+    constants_of_the_orders()
 
     for r in range(R):
         qx, sx, lc, lp, sb, ld = ["%s%d" % (n, r) for n in ("qx", "sx", "lc", "lp", "sb", "ld")]
-        prev = (rank - 1) % N
         arrival("qa%d" % r, 2 * inflow(prev, 1), [B(lp), half(lc, 0)])
         arrival("qb%d" % r, inflow(prev, 1), [half(lc, 1)])
         senders = [team * TEAM + j for j in range(TEAM) if j != m]
         if m == 0:
             senders += [(prev // TEAM) * TEAM + j for j in range(TEAM)]
-        came = arrival("va%d" % r, sum(inflow(s, TEAM) for s in senders), [B(ld, 0, 224) if m == 0 else B(ld, 16, 112)])
-        aown = B(ld, 224, 240) if m == 0 else B(ld, 0, 16)
+        came = arrival("va%d" % r, sum(inflow(s, TEAM) for s in senders), [B(ld, 0, 192), B(ld, 208, 240)])
 
-        quantise_state(r)
-
-        def own_column(k):
-            scan(half("DG", k), B("CD16"), half("AI", k), 0.0, A.add, A.min)
-
-        for h in range(2):
+        def vote(h):
             act(half("SBs", h), bank(2 * h))
             tt(half("AI", h), bank(2 * h + 1), half("SBs", h), A.is_ge)
-            if h:
-                own_column(2)
-            scan(half("AI", 2 + h), half("AI", h), half("AI", h), B("AI", C + H - 1, C + H) if h else 0.0, A.add, A.max)
-            own_column(h)
-        own_column(3)
-        ts(B(sb, 16, 48), B("DG", 15, 512, 16), plus2, None, A.add)
-        tt(B(sb, 0, 16), B("DG", C + 15, 512, 16), B("DG", 15, C, 16), A.subtract)
+
+        def whole(a, b):
+            scan(B("TS", a, b), B("AI", a, b), B("HALF", a, b), B("TS", a - 1, a) if a else 0.0, A.add, A.add)
+
+        def tails(h):
+            scan(half("HI", h), half("AI", h), B("PAST"), 0.0, A.add, A.min)
+            scan(half("HP", h), B("FROM"), half("AI", h), 0.0, A.min, A.add)
+
+        vote(0)
+        if r:
+            whole(0, H)
+        vote(1)
+        tails(0)
+        whole(H if r else 0, C)
+        tails(1)
+        for i in sorted(range(3), key=lambda i: RUNS[m][i]):
+            pair = [B("TS", 15, C, 16), B("H" + RUNS[m][i], 15, C, 16)]
+            tt(B(sb, 16 * i, 16 * i + 16), *(pair[::-1] if m == TEAM - 1 else pair), A.subtract)
         votes(r)
         ship(B(sx), B(lp), "qa%d" % r, False)
         ship(half(qx, 1), half(lc, 1), "qb%d" % r, True)
 
         if r == 0:
-            later_constants()
-            wait("y", came)
-            dma("y", T.wq[:].bitcast(dt.uint8), T.wc[:], [], [B("wq")])
+            constants_of_the_unpacking()
+            dma("y", T.wq[:].bitcast(dt.uint8), T.wc[:], [], [B("wq")], [came])
             dma("y", T.wp[:], T.ws[:], [], [B("wp")])
         if r == 1:
             dma("y", T.Vv[:], T.v[:], [B("X", 0, 4)], [B("Vv")])
         if r == R - 1:
             quant(B("vq"), B("vs"), B("Vv"))
-        cp(aown, B(sb, 16, 32))
-        tt(B("THP", wo, wo + 16), B("THR", wo, wo + 16), B(sb, 0, 16), A.subtract)
+        own = [B(sb, 16 * RUNS[m].index(k), 16 * RUNS[m].index(k) + 16) for k in "IP"]
+        tt(B("AT", 0, 16), *(own[::-1] if m == TEAM - 1 else own), A.is_gt)
         if m == 0:
-            if r == 0:
-                cp(B("THP", wp, wp + 16), B("THR", wp, wp + 16))
-        else:
-            tt(B("THP", wp, wp + 16), B("THR", wp, wp + 16), B(sb, 0, 16), A.subtract)
+            cp(B(ld, 192, 208), own[1])
+        if m == 1:
+            for h in range(2):
+                cp(B("LP", 16 * h, 16 * h + 16), own[1])
         for h in range(2):
             for b in range(4):
                 mm(bank(4 - 4 * h + b), piece("eq", b), piece("es", b), half(lc, h), half(lp, h))
             for b in range(4):
                 act(B("D", 512 * h + b, 512 * h + 512, 4), bank(4 - 4 * h + b))
 
-        if m == 0:
-            tt(B("S1", 0, 32), B(ld, 16, 48), B(ld, 80, 112), A.add)
-            tt(B("S1", 32, 48), B(ld, 144, 160), B(ld, 192, 208), A.add)
-            tt(B("S2", 16, 32), B("S1", 16, 32), B(ld, 160, 176), A.add)
-            tt(B("S2", 0, 16), B("S1", 0, 16), B("S1", 32, 48), A.add)
-            pair = B(ld, 208, 240)
-        else:
-            others = [i for i in range(TEAM) if i not in (m, m - 1)]
-            x1, x2 = [slot(k, m) + (16 if k < m else 0) for k in others]
-            tt(B("S1", 0, 16), B(ld, 32, 48), B(ld, x1, x1 + 16), A.add)
-            tt(B("S1", 16, 32), B(ld, x2, x2 + 16), B(ld, 16, 32), A.subtract)
-            tt(B("S2", 0, 16), B("S1", 0, 16), B(ld, x2, x2 + 16), A.add)
-            tt(B("S2", 16, 32), B("S1", 0, 16), B("S1", 16, 32), A.add)
-            pair = B(ld, 0, 32)
-        tt(B("GE"), B("S2"), B("THP"), A.is_ge)
-        tt(B("TI", 32, 64), B("GE"), pair, A.is_equal)
+        def run(a, n=32):
+            return B(ld, a, a + n)
+
+        plus, minus, before = (
+            ((run(16), run(80)), (run(144), run(192)), (run(160, 16), run(176, 16))),
+            ((run(0), run(64)), (run(96), B("LP")), (run(0, 16), run(16, 16))),
+            ((run(32), run(0)), (run(96), B(sb, 16, 48)), (run(32, 16), run(48, 16))),
+            ((run(64), run(0)), (B(sb, 0, 32), run(32)), (run(64, 16), run(80, 16))))[m]
+        tt(B("S1"), *plus, A.add)
+        tt(B("S2"), *minus, A.subtract)
+        tt(B("AT", 16, 32), *before, A.is_gt)
+        tt(B("GE"), B("S1"), B("S2"), A.is_ge)
+        tt(B("TI", 32, 64), B("GE"), B("AT"), A.is_equal)
         scan(B("TI", 1, 32), B("TI", 32, 63), B("MG", 0, 31), 0.0, A.add, A.mult)
+        tt(B("TK"), B("TI", 32, 64), B("KAP"), A.mult)
         tr(B("TO"), B("TI"))
+        tr(B("T1"), B("TK"))
         for h in range(2):
             scan(B("LO", 48 * h, 48 * h + 48), B("CK"), B("TO", 16 * h, 16 * h + 48), init, A.mult, A.add)
-        tt(B("T1"), B("TO", 32, 64), B("KAP"), A.mult)
         for h in range(2):
             tt(B("T2", 16 * h, 16 * h + 16), B("T1", 16 * h, 16 * h + 16), B("LO", 48 * h + 32, 48 * h + 48), A.subtract)
         tr(B("PW"), B("T2"))
         ts(B("PO"), B("PW"), qadd, None, A.add)
 
-        def minus_half(a, b, win, off):
-            o = B("HB", 4 * a, 4 * b)
+        def source(a, b):
+            return ("D", B("OFP", a // 4, b // 4)) if a < K else ("X", B("OFO", (a - K) // 4, (b - K) // 4))
+
+        def minus_half(a, b):
+            o, (win, off) = B("HB", 4 * a, 4 * b), source(a, b)
             op("s", lambda: S.activation(ap(o), T[win][:].indirect(ap(off)), COPY, scale=-0.5), [B(win), off], [o])
 
-        def zpart(a, b, win, off):
-            o, hb = B("Z", 4 * a, 4 * b), B("HB", 4 * ((a + H) % C), 4 * ((a + H) % C + b - a))
+        def zpart(a, b):
+            o, hb, (win, off) = B("Z", 4 * a, 4 * b), B("HB", 4 * ((a + H) % C), 4 * ((a + H) % C + b - a)), source(a, b)
             op("v", lambda: V.tensor_tensor(ap(o), T[win][:].indirect(ap(off)), ap(hb), A.add), [B(win), off, hb], [o])
 
-        for w, nn, a, b, dg, of in ((wo, "NO", 0, C - K, "DO", "OFO"), (wp, "NP", C - K, C, "DP", "OFP")):
-            op("v", lambda: V.tensor_copy(T[nn][:].indirect(ap(B("PO", w, w + 16))), T.IO[:]), [B("IO"), B("PO", w, w + 16)], [B(nn)])
-            if nn == "NP":
-                zpart(K, H, "X", B("OFO", 0, 8))
+        def scatter(nn, w):
+            off = B("PO", w, w + 16)
+            op("v", lambda: V.tensor_copy(T[nn][:].indirect(ap(off)), T.IO[:]), [B("IO"), off], [B(nn)])
+
+        def hold(dg, nn, a, b):
             scan(B(dg), B("CD4", 0, b - a), B(nn, a, b), 0.0, A.add, A.min)
-            if nn == "NP":
-                zpart(H + K, C, "X", B("OFO", 32, 40))
-            ts(B(of), B(dg, 3, b - a, 4), 4.0, oadd, A.mult, A.add)
-            if nn == "NO":
-                minus_half(H + K, C, "X", B("OFO", 32, 40))
-                minus_half(K, H, "X", B("OFO", 0, 8))
-                minus_half(H, H + K, "X", B("OFO", 8, 32))
-                if r == R - 1:
-                    dma("g", T.od[:], T.NO[0:128:16, :], [B("NO")], [])
-            else:
-                minus_half(0, K, "D", B("OFP"))
+
+        def offsets(of, dg):
+            ts(B(of), B(dg, 3, None, 4), 4.0, oadd, A.mult, A.add)
 
         def times32(a, b):
             act(B("Z32", 4 * a, 4 * b), B("Z", 4 * a, 4 * b), 32.0)
 
-        for h in range(2):
-            if h == 0:
-                zpart(0, K, "D", B("OFP"))
-            else:
-                zpart(H, H + K, "X", B("OFO", 8, 32))
+        def layer(h):
             quant(half("zq", h), half("zs", h), half("Z", h, 4))
-            if h == 0:
-                times32(0, H)
-                times32(H + K, C)
-            else:
-                times32(H, H + K)
             for b in range(4):
                 mm(bank(4 * h + b), piece("wq", b), piece("wp", b), half("zq", h), half("zs", h))
+
+        scatter("NO", 0)
+        hold("DO", "NO", 0, C - K)
+        offsets("OFO", "DO")
+        minus_half(H + K, C)
+        minus_half(K, H)
+        minus_half(H, H + K)
+        if r == R - 1:
+            dma("g", T.od[:], T.NO[0:128:16, :], [B("NO")], [])
+        scatter("NP", 16)
+        zpart(K, H)
+        hold("DP", "NP", C - K, C)
+        zpart(H + K, C)
+        offsets("OFP", "DP")
+        minus_half(0, K // 2)
+        minus_half(K // 2, K)
+        zpart(0, K)
+        zpart(H, H + K // 2)
+        layer(0)
+        times32(0, H)
+        times32(H + K, C)
+        zpart(H + K // 2, H + K)
+        times32(H, H + K)
+        layer(1)
+
         for h in range(2):
             for b in range(4):
                 rows = (512 * h + b, 512 * h + 512, 4)
                 tt(B("X32", *rows), bank(4 * h + b), B("Z32", *rows), A.add)
-                act(B("X", *rows), B("X32", *rows), 0.03125)
+                if (h, b) != (1, 3):
+                    act(B("X", *rows), B("X32", *rows), 0.03125)
+        for h in range(2):
+            quantise_state(r + 1, h)
+            if h == 0:
+                ts(B("X", *rows), B("X32", *rows), 0.03125, None, A.mult)
+            if r + 1 < R:
+                score(r + 1, h, 1)
+                score(r + 1, h, 0)
+            else:
+                mm(bank(h), B("vq"), B("vs"), half("qx%d" % R, h), half("sx%d" % R, h))
+                dma("y", T.oc[:, 512 * h:512 * h + 512], ap(half("qx%d" % R, h)).bitcast(dt.uint8), [half("qx%d" % R, h)], [])
 
-    quantise_state(R)
     sx = "sx%d" % R
     for k in range(4):
         dma("s" if k < 2 else "y", T.osc[4 * k:4 * k + 4, :], T[sx][32 * k:32 * k + 4, :], [B(sx)], [])
     for h in range(2):
         cp(half("YS", h), bank(h))
         dma("y" if h else "s", T.y[:, H * h:H * h + H], ap(half("YS", h)), [half("YS", h)], [])
-    g.wait_ge(T.sem.sent, sent[0])
-    for t in sorted(last.values()):
-        if waited.get(toks[t][0], 0) < toks[t][1]:
-            g.wait_ge(T.sem[toks[t][0]], toks[t][1])
+    moves = [c for c, call in enumerate(calls) if call[4] in ("soft", "hard")]
+    op("g", lambda: g.wait_ge(T.sem.sent, sent[0]), [], [], "c", moves)
+    issue()

@@ -18,11 +18,11 @@ SCRATCH = {
     "pi": _s(8, I32), "uo": _s(16, I32), "uo16": _s(16, U16), "IO": _s(256, BF), "I4": _s(160, BF), "I16": _s(128, BF),
     "PP": _s(16, F32), "TMP": _s(16, F32), "TM4": _s(320, BF), "NE": _s(128, BF),
     "HALF": _s(256, BF), "FROM": _s(128, BF), "PAST": _s(128, BF),
-    "CD4": _s(160, BF), "MG": _s(32, F32), "KAP": _s(32, F32), "CK": _s(48, F32),
+    "CD4": _s(160, BF), "KAP": _s(32, F32), "EVEN": _s(32, BF), "STEP": _s(128, BF), "IR": _s(256, BF),
     "SBs": _s(256, F32), "AI": _s(256, BF), "TS": _s(256, BF), "HP": _s(256, BF), "HI": _s(256, BF),
-    "LP": _s(32, BF), "AT": _s(32, BF),
-    "S1": _s(32, F32), "S2": _s(32, F32), "GE": _s(32, F32), "TI": _s(64, F32), "TO": _s(64, F32), "LO": _s(96, F32),
-    "ONE": _s(256, BF), "TK": _s(32, F32), "T1": _s(32, F32), "T2": _s(32, F32), "PW": _s(32, F32), "PO": _s(32, U16),
+    "AT": _s(32, BF),
+    "S1": _s(32, F32), "S2": _s(32, F32), "GE": _s(32, F32), "TI": _s(320, BF), "TO": _s(384, BF), "LO": _s(192, BF),
+    "ONE": _s(256, BF), "FL": _s(32, BF), "PW": _s(64, BF), "PO": _s(32, U16),
     "NO": _s(256, BF), "NP": _s(256, BF), "DO": _s(160, BF), "DP": _s(96, BF), "OFO": _s(40, U16), "OFP": _s(24, U16),
     "YS": _s(256, F32),
     "ps": ("psum", [128, 4096], F32),
@@ -33,8 +33,8 @@ for _r in range(R + 1):
 for _r in range(R):
     SCRATCH["lc%d" % _r] = _s(256, FP8)
     SCRATCH["lp%d" % _r] = _s(256, U8)
-    SCRATCH["sb%d" % _r] = _s(48, BF)
-    SCRATCH["ld%d" % _r] = _s(240, BF)
+    SCRATCH["sb%d" % _r] = _s(32, BF)
+    SCRATCH["ld%d" % _r] = _s(256, BF)
 SHARED = ["k%d" % i for i in range(120)]
 ONCE = ["d%d" % i for i in range(16)]
 SEMAPHORES = SHARED + ONCE + ["sent"]
@@ -42,8 +42,6 @@ SEMAPHORES += ["%s%d" % (n, r) for n in ("va", "qa", "qb") for r in range(R)]
 
 A = AluOpType
 COPY = ActivationFunctionType.Copy
-
-RUNS = ("IIP", "IIP", "IPP", "PPI")
 
 
 def rank_program(g, core, T, topo):
@@ -207,13 +205,9 @@ def rank_program(g, core, T, topo):
 
     def votes(r):
         sb, ld = "sb%d" % r, "ld%d" % r
-        plan = []
-        for j in range(TEAM):
-            if j != m:
-                want = "IP" if j == m + 1 else "II" if j > m else "PP" if j else RUNS[m][1:] if m < TEAM - 1 else "PP"
-                plan.append((team * TEAM + j, 16 * RUNS[m].index(want), 32 * m if j else 64 * (m - 1), 32))
+        plan = [(team * TEAM + j, 0, 32 * m, 32) for j in range(TEAM) if j != m]
         narrow = r == 0 and m == 1
-        plan.append((((team + 1) * TEAM) % N, 16 if m == TEAM - 1 else 0, (32, 96, 208, 160)[m], 16 if narrow else 32))
+        plan.append((((team + 1) * TEAM) % N, 0, 128 + 32 * m, 16 if narrow else 32))
         trs = []
         for i, (d, a, b, w) in enumerate(plan):
             rid, pid = topo.addr(T.cores[d], core)
@@ -228,7 +222,7 @@ def rank_program(g, core, T, topo):
     def inflow(src, share):
         return len(topo.engines(T.cores[src], core)) // share
 
-    p_, q_, u_, t_, low, qadd, init, u1, ufix, oadd = [B("PP", i, i + 1) for i in range(10)]
+    p_, row, u_, t_, odd, sign, top, q_, low, init, u1, ufix, oadd, jump, first = [B("PP", i, i + 1) for i in range(15)]
 
     dma("y", T.X[:, 0:512], T.x[:, 0:512], [], [half("X", 0, 4)])
     dma("y", T.U[:], T.u[:], [], [B("U")])
@@ -239,15 +233,19 @@ def rank_program(g, core, T, topo):
     iota(B("I4"), [[0, 40], [1, 4]])
     fill(B("ONE"), 1.0)
     fill(B("ET"), 0.0)
-    fill(B("HALF"), -0.5)
-    scan(B("IO"), B("ONE"), B("ONE"), -1.0, A.add, A.mult)
     ts(B("pi", 1, 2), B("pi", 0, 1), 15, None, A.bitwise_and)
     ts(B("pi", 2, 3), B("pi", 0, 1), 2, 3, A.arith_shift_right, A.bitwise_and)
     ts(B("pi", 3, 4), B("pi", 0, 1), 3, None, A.bitwise_and)
+    ts(B("pi", 4, 5), B("pi", 0, 1), 4, 1, A.arith_shift_right, A.bitwise_and)
+    fill(B("HALF"), -0.5)
+    scan(B("IO"), B("ONE"), B("ONE"), -1.0, A.add, A.mult)
+    cp(B("PP", 0, 5), B("pi", 0, 5))
     cp(B("uo16"), B("uo"))
-    fill(B("MG"), 1.0)
-    fill(B("CK"), 1.0)
-    cp(B("PP", 0, 4), B("pi", 0, 4))
+    fill(B("TO"), 0.0)
+    ts(sign, odd, -2.0, 1.0, A.mult, A.add)
+    ts(top, odd, 15.0, None, A.mult)
+    fill(B("TI"), 0.0)
+    ts(q_, row, sign, top, A.mult, A.add)
 
     def constants_of_the_votes():
         ts(low, q_, 0.5, -8.0, A.mult, A.add)
@@ -272,18 +270,23 @@ def rank_program(g, core, T, topo):
         ts(B("TM4", 160, 320), B("I4"), u1, -256.0, A.is_equal, A.mult)
 
     def constants_of_the_unpacking():
-        for b in range(4):
-            quant(piece("eq", b), piece("es", b), B("ET", 3 - b, 515 - b))
-        fill(B("TI", 0, 1), 0.0)
-        fill(B("MG", 15, 16), 0.0)
-        fill(B("CK", 16, 17), 4096.0)
-        fill(B("CK", 32, 33), 1.0 / 4096)
-        ts(qadd, q_, 0.25, None, A.add)
-        ts(init, q_, -16.0, None, A.mult)
-        tt(oadd, t_, ufix, A.add)
-        for h in range(2):
-            ts(B("KAP", 16 * h, 16 * h + 16), B("TMP"), q_, None, A.subtract)
+        ts(jump, odd, 32.0, None, A.mult)
+        ts(first, top, -1.0, -1.0, A.mult, A.add)
+        quant(piece("eq", 0), piece("es", 0), B("ET", 3, 515))
+        quant(piece("eq", 1), piece("es", 1), B("ET", 2, 514))
+        ts(B("NE"), B("I16"), 0.0, jump, A.is_equal, A.mult)
+        quant(piece("eq", 2), piece("es", 2), B("ET", 1, 513))
+        quant(piece("eq", 3), piece("es", 3), B("ET", 0, 512))
+        ts(B("STEP"), B("NE"), sign, None, A.add)
         tt(B("CD4"), B("TM4", 0, 160), B("TM4", 160, 320), A.add)
+        scan(half("IR", 0), B("STEP"), half("ONE", 0), first, A.add, A.mult)
+        ts(init, row, 16.0, None, A.mult)
+        tt(oadd, t_, ufix, A.add)
+        ts(B("KAP", 0, 16), B("TMP"), q_, None, A.subtract)
+        ts(B("KAP", 16, 32), B("TMP"), q_, 1.0, A.subtract, A.subtract)
+        ts(B("EVEN", 0, 16), B("ONE", 0, 16), odd, None, A.subtract)
+        ts(B("EVEN", 16, 32), B("ONE", 0, 16), odd, None, A.mult)
+        scan(half("IR", 1), B("STEP"), half("ONE", 0), B("IR", H - 1, H), A.add, A.mult)
 
     def quantise_state(r, h):
         qx, sx = "qx%d" % r, "sx%d" % r
@@ -313,11 +316,14 @@ def rank_program(g, core, T, topo):
         senders = [team * TEAM + j for j in range(TEAM) if j != m]
         if m == 0:
             senders += [(prev // TEAM) * TEAM + j for j in range(TEAM)]
-        came = arrival("va%d" % r, sum(inflow(s, TEAM) for s in senders), [B(ld, 0, 192), B(ld, 208, 240)])
+        came = arrival("va%d" % r, sum(inflow(s, TEAM) for s in senders), [B(ld)])
 
         def vote(h):
-            act(half("SBs", h), bank(2 * h))
-            tt(half("AI", h), bank(2 * h + 1), half("SBs", h), A.is_ge)
+            n = H // 2 if h and r else H
+            for a in range(0, H, n):
+                act(B("SBs", H * h + a, H * h + a + n), B("ps", 1024 * h + a, 1024 * h + a + n))
+            for a in range(0, H, n):
+                tt(B("AI", H * h + a, H * h + a + n), B("ps", 1024 * h + 512 + a, 1024 * h + 512 + a + n), B("SBs", H * h + a, H * h + a + n), A.is_ge)
 
         def whole(a, b):
             scan(B("TS", a, b), B("AI", a, b), B("HALF", a, b), B("TS", a - 1, a) if a else 0.0, A.add, A.add)
@@ -333,8 +339,8 @@ def rank_program(g, core, T, topo):
         tails(0)
         whole(H if r else 0, C)
         tails(1)
-        for i in sorted(range(3), key=lambda i: RUNS[m][i]):
-            pair = [B("TS", 15, C, 16), B("H" + RUNS[m][i], 15, C, 16)]
+        for i, tail in enumerate(("HI", "HP")):
+            pair = [B("TS", 15, C, 16), B(tail, 15, C, 16)]
             tt(B(sb, 16 * i, 16 * i + 16), *(pair[::-1] if m == TEAM - 1 else pair), A.subtract)
         votes(r)
         ship(B(sx), B(lp), "qa%d" % r, False)
@@ -348,57 +354,67 @@ def rank_program(g, core, T, topo):
             dma("y", T.Vv[:], T.v[:], [B("X", 0, 4)], [B("Vv")])
         if r == R - 1:
             quant(B("vq"), B("vs"), B("Vv"))
-        own = [B(sb, 16 * RUNS[m].index(k), 16 * RUNS[m].index(k) + 16) for k in "IP"]
-        tt(B("AT", 0, 16), *(own[::-1] if m == TEAM - 1 else own), A.is_gt)
-        if m == 0:
-            cp(B(ld, 192, 208), own[1])
-        if m == 1:
-            for h in range(2):
-                cp(B("LP", 16 * h, 16 * h + 16), own[1])
+
+        def sums(k, kind, far):
+            name, a = (sb, 0) if k == m and not far else (ld, 128 * far + 32 * k)
+            return B(name, a + 16 * kind, a + 16 * kind + 16)
+
+        def sign_of_votes(w):
+            k = (m - w) % TEAM
+            pair = [sums(k, kind, w > m) for kind in (0, 1)]
+            tt(B("AT", 16 * w, 16 * w + 16), *(pair[::-1] if k == TEAM - 1 else pair), A.is_gt)
+
+        sign_of_votes(0)
         for h in range(2):
             for b in range(4):
                 mm(bank(4 - 4 * h + b), piece("eq", b), piece("es", b), half(lc, h), half(lp, h))
             for b in range(4):
                 act(B("D", 512 * h + b, 512 * h + 512, 4), bank(4 - 4 * h + b))
 
-        def run(a, n=32):
-            return B(ld, a, a + n)
+        def sub(v, a, n=16):
+            a += v[1].start or 0
+            return B(v[0], a, a + n)
 
-        plus, minus, before = (
-            ((run(16), run(80)), (run(144), run(192)), (run(160, 16), run(176, 16))),
-            ((run(0), run(64)), (run(96), B("LP")), (run(0, 16), run(16, 16))),
-            ((run(32), run(0)), (run(96), B(sb, 16, 48)), (run(32, 16), run(48, 16))),
-            ((run(64), run(0)), (B(sb, 0, 32), run(32)), (run(64, 16), run(80, 16))))[m]
-        tt(B("S1"), *plus, A.add)
-        tt(B("S2"), *minus, A.subtract)
-        tt(B("AT", 16, 32), *before, A.is_gt)
-        tt(B("GE"), B("S1"), B("S2"), A.is_ge)
-        tt(B("TI", 32, 64), B("GE"), B("AT"), A.is_equal)
-        scan(B("TI", 1, 32), B("TI", 32, 63), B("MG", 0, 31), 0.0, A.add, A.mult)
-        tt(B("TK"), B("TI", 32, 64), B("KAP"), A.mult)
-        tr(B("TO"), B("TI"))
-        tr(B("T1"), B("TK"))
-        for h in range(2):
-            scan(B("LO", 48 * h, 48 * h + 48), B("CK"), B("TO", 16 * h, 16 * h + 48), init, A.mult, A.add)
-        for h in range(2):
-            tt(B("T2", 16 * h, 16 * h + 16), B("T1", 16 * h, 16 * h + 16), B("LO", 48 * h + 32, 48 * h + 48), A.subtract)
-        tr(B("PW"), B("T2"))
-        ts(B("PO"), B("PW"), qadd, None, A.add)
+        def places(w):
+            s1, s2, ge, at, po = [B(n, 16 * w, 16 * w + 16) for n in ("S1", "S2", "GE", "AT", "PO")]
+            ti, to, lo, pw, f = B("TI", 160 * w), 192 * w, 96 * w, B("PW", 32 * w), B("FL", 16 * w, 16 * w + 16)
+            x = [sums(k, int(k >= (m - w) % TEAM), w > m) for k in range(TEAM)]
+            return [
+                lambda: (tt(s1, x[0], x[1], A.add), tt(s2, x[3], x[2], A.subtract), w and sign_of_votes(1)),
+                lambda: tt(ge, s1, s2, A.is_ge),
+                lambda: tt(f, ge, at, A.is_equal),
+                lambda: (scan(sub(ti, 1, 15), sub(f, 0, 15), B("EVEN", 0, 15), 0.0, A.add, A.mult),
+                         scan(sub(ti, 65, 15), sub(f, 0, 15), B("EVEN", 16, 31), 0.0, A.add, A.mult),
+                         tt(sub(ti, 32), f, B("KAP", 0, 16), A.mult),
+                         tt(sub(ti, 128), f, B("KAP", 16, 32), A.mult)),
+                lambda: tr(B("TO", to, to + 160), sub(ti, 0, 160)),
+                lambda: (scan(B("LO", lo + 1, lo + 48), B("TO", to + 97, to + 144), B("TO", to, to + 47), init, A.add, A.subtract),
+                         scan(B("LO", lo + 94, lo + 47, -1), B("TO", to + 190, to + 143, -1), B("TO", to + 95, to + 48, -1),
+                              init, A.add, A.subtract)),
+                lambda: tr(sub(pw, 0, 32), B("LO", lo + 32, lo + 64)),
+                lambda: ts(po, sub(pw, 0), q_, None, A.add)]
+
+        for mine, theirs in zip(places(0), places(1)):
+            mine()
+            theirs()
 
         def source(a, b):
             return ("D", B("OFP", a // 4, b // 4)) if a < K else ("X", B("OFO", (a - K) // 4, (b - K) // 4))
 
-        def minus_half(a, b):
+        def minus_half(a, b, q="s"):
             o, (win, off) = B("HB", 4 * a, 4 * b), source(a, b)
-            op("s", lambda: S.activation(ap(o), T[win][:].indirect(ap(off)), COPY, scale=-0.5), [B(win), off], [o])
+            if q == "s":
+                op("s", lambda: S.activation(ap(o), T[win][:].indirect(ap(off)), COPY, scale=-0.5), [B(win), off], [o])
+            else:
+                op("v", lambda: V.tensor_scalar(ap(o), T[win][:].indirect(ap(off)), -0.5, None, A.mult), [B(win), off], [o])
 
         def zpart(a, b):
             o, hb, (win, off) = B("Z", 4 * a, 4 * b), B("HB", 4 * ((a + H) % C), 4 * ((a + H) % C + b - a)), source(a, b)
             op("v", lambda: V.tensor_tensor(ap(o), T[win][:].indirect(ap(off)), ap(hb), A.add), [B(win), off, hb], [o])
 
-        def scatter(nn, w):
-            off = B("PO", w, w + 16)
-            op("v", lambda: V.tensor_copy(T[nn][:].indirect(ap(off)), T.IO[:]), [B("IO"), off], [B(nn)])
+        def scatter(nn, a, b):
+            off, j = B("PO", a, b), B("IR", 16 * (a % 16), 16 * (a % 16 + b - a))
+            op("v", lambda: V.tensor_copy(T[nn][:].indirect(ap(off)), ap(j)), [j, off], [B(nn)])
 
         def hold(dg, nn, a, b):
             scan(B(dg), B("CD4", 0, b - a), B(nn, a, b), 0.0, A.add, A.min)
@@ -414,21 +430,22 @@ def rank_program(g, core, T, topo):
             for b in range(4):
                 mm(bank(4 * h + b), piece("wq", b), piece("wp", b), half("zq", h), half("zs", h))
 
-        scatter("NO", 0)
+        scatter("NO", 0, 16)
+        scatter("NP", 16, 20)
         hold("DO", "NO", 0, C - K)
         offsets("OFO", "DO")
         minus_half(H + K, C)
-        minus_half(K, H)
         minus_half(H, H + K)
         if r == R - 1:
             dma("g", T.od[:], T.NO[0:128:16, :], [B("NO")], [])
-        scatter("NP", 16)
-        zpart(K, H)
+        scatter("NP", 20, 32)
+        minus_half(K, H, "v")
         hold("DP", "NP", C - K, C)
-        zpart(H + K, C)
+        zpart(K, H)
         offsets("OFP", "DP")
         minus_half(0, K // 2)
         minus_half(K // 2, K)
+        zpart(H + K, C)
         zpart(0, K)
         zpart(H, H + K // 2)
         layer(0)
@@ -457,7 +474,7 @@ def rank_program(g, core, T, topo):
 
     sx = "sx%d" % R
     for k in range(4):
-        dma("s" if k < 2 else "y", T.osc[4 * k:4 * k + 4, :], T[sx][32 * k:32 * k + 4, :], [B(sx)], [])
+        dma("s", T.osc[4 * k:4 * k + 4, :], T[sx][32 * k:32 * k + 4, :], [B(sx)], [])
     for h in range(2):
         cp(half("YS", h), bank(h))
         dma("y" if h else "s", T.y[:, H * h:H * h + H], ap(half("YS", h)), [half("YS", h)], [])

@@ -3,6 +3,9 @@ from concourse.mybir import dt, AluOpType, ActivationFunctionType
 
 C, K, R, TEAM = 256, 96, 3, 4
 H = C // 2
+NS = 7
+RUN = 16 * NS
+ROUND = 49152.0
 FP8, U8, BF, F32, I32, U16 = "float8_e4m3fn_x4", "uint8", "bfloat16", "float32", "int32", "uint16"
 
 
@@ -15,14 +18,13 @@ SCRATCH = {
     "U": _s(512, BF), "Vv": _s(512, BF), "uq": _s(128, FP8), "us": _s(128, U8), "up": _s(256, FP8), "ups": _s(256, U8),
     "vq": _s(128, FP8), "vs": _s(128, U8), "wq": _s(512, FP8), "wp": _s(512, U8), "zq": _s(256, FP8), "zs": _s(256, U8),
     "ET": _s(520, BF), "eq": _s(512, FP8), "es": _s(512, U8),
-    "pi": _s(8, I32), "uo": _s(16, I32), "uo16": _s(16, U16), "IO": _s(256, BF), "I4": _s(160, BF), "I16": _s(128, BF),
-    "PP": _s(16, F32), "TMP": _s(16, F32), "TM4": _s(320, BF), "NE": _s(128, BF),
+    "pi": _s(8, I32), "uo": _s(16, I32), "uo16": _s(16, U16), "IO": _s(256, BF), "I16": _s(128, BF),
+    "PP": _s(24, F32), "TMP": _s(16, F32), "NE": _s(128, BF),
     "HALF": _s(256, BF), "FROM": _s(128, BF), "PAST": _s(128, BF),
-    "CD4": _s(160, BF), "KAP": _s(32, F32), "EVEN": _s(32, BF), "STEP": _s(128, BF), "IR": _s(256, BF),
+    "CD4": _s(160, BF), "MUL": _s(8 * RUN, BF), "ADD": _s(2 * RUN, "float16"), "STEP": _s(128, BF), "IR": _s(256, BF),
     "SBs": _s(256, F32), "AI": _s(256, BF), "TS": _s(256, BF), "HP": _s(256, BF), "HI": _s(256, BF),
-    "AT": _s(32, BF),
-    "S1": _s(32, F32), "S2": _s(32, F32), "GE": _s(32, F32), "TI": _s(320, BF), "TO": _s(384, BF), "LO": _s(192, BF),
-    "ONE": _s(256, BF), "FL": _s(32, BF), "PW": _s(64, BF), "PO": _s(32, U16),
+    "MORE": _s(16, BF), "TI": _s(20 * RUN, BF), "TO": _s(384, BF), "LO": _s(192, BF),
+    "ONE": _s(256, BF), "PW": _s(64, BF), "PO": _s(32, U16),
     "NO": _s(256, BF), "NP": _s(256, BF), "DO": _s(160, BF), "DP": _s(96, BF), "OFO": _s(40, U16), "OFP": _s(24, U16),
     "YS": _s(256, F32),
     "ps": ("psum", [128, 4096], F32),
@@ -38,7 +40,7 @@ for _r in range(R):
 SHARED = ["k%d" % i for i in range(120)]
 ONCE = ["d%d" % i for i in range(16)]
 SEMAPHORES = SHARED + ONCE + ["sent"]
-SEMAPHORES += ["%s%d" % (n, r) for n in ("va", "qa", "qb") for r in range(R)]
+SEMAPHORES += ["%s%d" % (n, r) for n in ("va", "vb", "qa", "qb") for r in range(R)]
 
 A = AluOpType
 COPY = ActivationFunctionType.Copy
@@ -175,6 +177,11 @@ def rank_program(g, core, T, topo):
     def act(o, a, scale=1.0):
         return op("s", lambda: S.activation(ap(o), ap(a), COPY, scale=scale), [a], [o])
 
+    def lin(o, a, scale, bias):
+        rd = [a] + [s for s in (scale, bias) if isinstance(s, tuple)]
+        a1, a2 = [ap(s) if isinstance(s, tuple) else s for s in (scale, bias)]
+        return op("s", lambda: S.activation(ap(o), ap(a), ActivationFunctionType.Identity, bias=a2, scale=a1), rd, [o])
+
     def mm(o, lc, ls, rc, rs):
         return op("t", lambda: g.tensor.matmul_mx(ap(o), ap(lc), ap(ls), ap(rc), ap(rs), True, True), [lc, ls, rc, rs], [o])
 
@@ -203,20 +210,29 @@ def rank_program(g, core, T, topo):
         op("g", lambda: g.remote_dma(b, a, T.sem[sem], T.sem.sent, pid, rid, topo.mask(core, nxt)), [src], [])
         sent[0] += len(topo.engines(core, nxt))
 
+    def single(k):
+        return k + 1 if k + 1 < TEAM else k - 1
+
+    first_run = (0, 1) if m < 2 else (1, 0)
+
     def votes(r):
         sb, ld = "sb%d" % r, "ld%d" % r
-        plan = [(team * TEAM + j, 0, 32 * m, 32) for j in range(TEAM) if j != m]
-        narrow = r == 0 and m == 1
-        plan.append((((team + 1) * TEAM) % N, 0, 128 + 32 * m, 16 if narrow else 32))
-        trs = []
-        for i, (d, a, b, w) in enumerate(plan):
-            rid, pid = topo.addr(T.cores[d], core)
-            es = topo.engines(core, T.cores[d])
-            n = len(es) // TEAM
-            trs.append((RemoteDMATransfer(dst_ids=[DstId(rid=rid, pnc=pid)], dma_engine_mask=bits(es[n * i:n * i + n]),
-                                          remote_sem=T.sem["va%d" % r], src=ap(B(sb, a, a + w)), dst=ap(B(ld, b, b + w))), B(sb, a, a + w)))
+
+        def run(to, kinds, base, sem, share, i):
+            rid, pid = topo.addr(T.cores[to], core)
+            es = topo.engines(core, T.cores[to])
+            n = len(es) // share
+            a, b = 16 * kinds[0], 16 * kinds[-1] + 16
             sent[0] += n
-        for part in ([trs[-1:], trs[:-1]] if narrow else [trs]):
+            return (RemoteDMATransfer(dst_ids=[DstId(rid=rid, pnc=pid)], dma_engine_mask=bits(es[n * i:n * i + n]),
+                                      remote_sem=T.sem[sem], src=ap(B(sb, a, b)), dst=ap(B(ld, base + a, base + b))), B(sb, a, b))
+
+        def mate(j, share, i):
+            return run(team * TEAM + j, (0, 1) if j == m + 1 else (int(j < m),), 32 * m, ("vb%d" if share == 1 else "va%d") % r, share, i)
+
+        two = [mate(j, 2, i) for i, j in enumerate(j for j in range(TEAM) if j not in (m, single(m)))]
+        far = run(((team + 1) * TEAM) % N, (0, 1) if m == TEAM - 1 else (0,), 128 + 32 * m, "vb%d" % r, 1, 0)
+        for part in (two, [mate(single(m), 1, 0)], [far]):
             op("g", lambda part=part: g.remote_dma_fused([t for t, _ in part], local_sem=T.sem.sent), [v for _, v in part], [])
 
     def inflow(src, share):
@@ -230,31 +246,18 @@ def rank_program(g, core, T, topo):
     iota(B("pi", 0, 1), [[0, 1]], 1)
     iota(B("uo"), [[1, 2], [16, 8]])
     iota(B("I16"), [[0, 8], [1, 16]])
-    iota(B("I4"), [[0, 40], [1, 4]])
     fill(B("ONE"), 1.0)
     fill(B("ET"), 0.0)
     ts(B("pi", 1, 2), B("pi", 0, 1), 15, None, A.bitwise_and)
     ts(B("pi", 2, 3), B("pi", 0, 1), 2, 3, A.arith_shift_right, A.bitwise_and)
     ts(B("pi", 3, 4), B("pi", 0, 1), 3, None, A.bitwise_and)
     ts(B("pi", 4, 5), B("pi", 0, 1), 4, 1, A.arith_shift_right, A.bitwise_and)
-    fill(B("HALF"), -0.5)
-    scan(B("IO"), B("ONE"), B("ONE"), -1.0, A.add, A.mult)
-    cp(B("PP", 0, 5), B("pi", 0, 5))
     cp(B("uo16"), B("uo"))
-    fill(B("TO"), 0.0)
-    ts(sign, odd, -2.0, 1.0, A.mult, A.add)
-    ts(top, odd, 15.0, None, A.mult)
-    fill(B("TI"), 0.0)
-    ts(q_, row, sign, top, A.mult, A.add)
-
-    def constants_of_the_votes():
-        ts(low, q_, 0.5, -8.0, A.mult, A.add)
-        ts(B("NE"), B("I16"), q_, 1024.0, A.not_equal, A.mult)
-        ts(u1, u_, 1.0, None, A.add)
-
-    def patterns_of_the_votes():
-        ts(B("FROM"), B("NE"), low, None, A.add)
-        ts(B("PAST"), B("NE"), low, 0.5, A.add, A.add)
+    cp(B("PP", 0, 5), B("pi", 0, 5))
+    lin(sign, odd, -2.0, 1.0)
+    lin(top, odd, 15.0, 0.0)
+    lin(u1, u_, 1.0, 1.0)
+    lin(q_, row, sign, top)
 
     def deciding_columns(k):
         off = B("uo16", 8 * k, 8 * k + 8)
@@ -265,28 +268,39 @@ def rank_program(g, core, T, topo):
     def constants_of_the_orders():
         ts(B("ET", 3, 515, 4), B("IO", 0, 128), p_, None, A.is_equal)
         ts(ufix, u_, 3.0, 1024.0, A.is_lt, A.mult)
-        ts(B("TMP"), B("IO", 0, 16), -16.0, 256.0, A.mult, A.add)
-        ts(B("TM4", 0, 160), B("I4"), u_, 1024.0, A.is_equal, A.mult)
-        ts(B("TM4", 160, 320), B("I4"), u1, -256.0, A.is_equal, A.mult)
+        ts(B("TMP", 0, 4), B("IO", 0, 4), u_, 1024.0, A.is_equal, A.mult)
+        ts(B("TMP", 4, 8), B("IO", 0, 4), u1, -256.0, A.is_equal, A.mult)
+        ts(B("FROM"), B("NE"), low, None, A.add)
+        ts(B("PAST"), B("NE"), low, 0.5, A.add, A.add)
 
     def constants_of_the_unpacking():
-        ts(jump, odd, 32.0, None, A.mult)
-        ts(first, top, -1.0, -1.0, A.mult, A.add)
-        quant(piece("eq", 0), piece("es", 0), B("ET", 3, 515))
-        quant(piece("eq", 1), piece("es", 1), B("ET", 2, 514))
-        ts(B("NE"), B("I16"), 0.0, jump, A.is_equal, A.mult)
-        quant(piece("eq", 2), piece("es", 2), B("ET", 1, 513))
-        quant(piece("eq", 3), piece("es", 3), B("ET", 0, 512))
-        ts(B("STEP"), B("NE"), sign, None, A.add)
-        tt(B("CD4"), B("TM4", 0, 160), B("TM4", 160, 320), A.add)
-        scan(half("IR", 0), B("STEP"), half("ONE", 0), first, A.add, A.mult)
-        ts(init, row, 16.0, None, A.mult)
-        tt(oadd, t_, ufix, A.add)
-        ts(B("KAP", 0, 16), B("TMP"), q_, None, A.subtract)
-        ts(B("KAP", 16, 32), B("TMP"), q_, 1.0, A.subtract, A.subtract)
-        ts(B("EVEN", 0, 16), B("ONE", 0, 16), odd, None, A.subtract)
-        ts(B("EVEN", 16, 32), B("ONE", 0, 16), odd, None, A.mult)
-        scan(half("IR", 1), B("STEP"), half("ONE", 0), B("IR", H - 1, H), A.add, A.mult)
+        tt(B("TMP", 8, 12), B("TMP", 0, 4), B("TMP", 4, 8), A.add)
+        lin(B("STEP"), half("ONE", 0), sign, 0.0)
+        lin(jump, odd, 30.0, 1.0)
+        lin(first, odd, -15.0, -1.0)
+        lin(init, row, 32.0, 0.0)
+        for i in range(2):
+            lin(B("PP", 16 + i, 17 + i), q_, -1024.0, 1024.0 * (C - i))
+            lin(B("PP", 18 + i, 19 + i), odd, 1024.0 * (2 * i - 1), 1024.0 * (1 - i))
+        for step, c in enumerate((0.0, 1024.0, 1.0, 2.0 ** -18, 1.0)):
+            act(B("MUL", step, None, NS), B("ONE", 0, 128), c)
+        lin(B("STEP", 0, H, 16), B("ONE", 0, 8), jump, 0.0)
+        for step, c in ((3, ROUND), (4, -ROUND), (5, 0.0), (6, 0.0)):
+            ts(B("ADD", step, None, NS), B("ONE", 0, 32), c, None, A.mult)
+        for w in range(2):
+            last = [B("MUL", RUN * (4 * w + i) + NS - 1, RUN * (4 * w + i + 1), NS) for i in range(4)]
+            for i in range(2):
+                lin(last[i], B("IO", 0, 16), -16384.0, B("PP", 16 + i, 17 + i))
+                lin(last[2 + i], B("ONE", 0, 16), B("PP", 18 + i, 19 + i), 0.0)
+            act(B("TI", 10 * RUN * w + NS - 1, 10 * RUN * (w + 1), NS), B("ONE", 0, 160), 0.0)
+            act(B("TO", 192 * w + 160, 192 * w + 192), B("ONE", 0, 32), 0.0)
+        lin(oadd, t_, 1.0, ufix)
+        for k in range(4):
+            lin(B("CD4", k, None, 4), B("ONE", 0, 40), B("TMP", 8 + k, 9 + k), 0.0)
+        for b in range(4):
+            quant(piece("eq", b), piece("es", b), B("ET", 3 - b, 515 - b))
+            if b % 2:
+                scan(half("IR", b // 2), B("STEP"), half("ONE", 0), B("IR", H - 1, H) if b // 2 else first, A.add, A.mult)
 
     def quantise_state(r, h):
         qx, sx = "qx%d" % r, "sx%d" % r
@@ -298,12 +312,14 @@ def rank_program(g, core, T, topo):
         mm(bank(2 * h + 1 - k), piece("up", k), piece("ups", k), half("qx%d" % r, h), half("sx%d" % r, h))
 
     quantise_state(0, 0)
-    constants_of_the_votes()
+    scan(B("IO"), B("ONE"), B("ONE"), -1.0, A.add, A.mult)
     quant(B("uq"), B("us"), B("U"))
-    patterns_of_the_votes()
+    fill(B("HALF"), -0.5)
     deciding_columns(1)
     quantise_state(0, 1)
     deciding_columns(0)
+    ts(B("NE"), B("I16"), q_, 1024.0, A.not_equal, A.mult)
+    lin(low, q_, 0.5, -8.0)
     for k in (1, 0):
         for h in range(2):
             score(0, h, k)
@@ -313,13 +329,15 @@ def rank_program(g, core, T, topo):
         qx, sx, lc, lp, sb, ld = ["%s%d" % (n, r) for n in ("qx", "sx", "lc", "lp", "sb", "ld")]
         arrival("qa%d" % r, 2 * inflow(prev, 1), [B(lp), half(lc, 0)])
         arrival("qb%d" % r, inflow(prev, 1), [half(lc, 1)])
-        senders = [team * TEAM + j for j in range(TEAM) if j != m]
-        if m == 0:
-            senders += [(prev // TEAM) * TEAM + j for j in range(TEAM)]
-        came = arrival("va%d" % r, sum(inflow(s, TEAM) for s in senders), [B(ld)])
+        soon, late = [[k for k in range(TEAM) if k != m and (single(k) == m) == alone] for alone in (False, True)]
+        came = arrival("va%d" % r, sum(inflow(team * TEAM + k, 2) for k in soon), [B(ld, 32 * k, 32 * k + 32) for k in soon])
+        if m:
+            arrival("vb%d" % r, sum(inflow(team * TEAM + k, 1) for k in late), [B(ld, 32 * k, 32 * k + 32) for k in late])
+        else:
+            arrival("vb%d" % r, sum(inflow(prev - i, 1) for i in range(TEAM)), [B(ld, 128, 256)])
 
         def vote(h):
-            n = H // 2 if h and r else H
+            n = H // 2
             for a in range(0, H, n):
                 act(B("SBs", H * h + a, H * h + a + n), B("ps", 1024 * h + a, 1024 * h + a + n))
             for a in range(0, H, n):
@@ -328,19 +346,22 @@ def rank_program(g, core, T, topo):
         def whole(a, b):
             scan(B("TS", a, b), B("AI", a, b), B("HALF", a, b), B("TS", a - 1, a) if a else 0.0, A.add, A.add)
 
-        def tails(h):
-            scan(half("HI", h), half("AI", h), B("PAST"), 0.0, A.add, A.min)
-            scan(half("HP", h), B("FROM"), half("AI", h), 0.0, A.min, A.add)
+        def tails(a, b):
+            for kind in first_run:
+                if kind:
+                    scan(B("HP", a, b), B("FROM", 0, b - a), B("AI", a, b), 0.0, A.min, A.add)
+                else:
+                    scan(B("HI", a, b), B("AI", a, b), B("PAST", 0, b - a), 0.0, A.add, A.min)
 
         vote(0)
         if r:
             whole(0, H)
         vote(1)
-        tails(0)
+        tails(0, H)
         whole(H if r else 0, C)
-        tails(1)
-        for i, tail in enumerate(("HI", "HP")):
-            pair = [B("TS", 15, C, 16), B(tail, 15, C, 16)]
+        tails(H, C)
+        for i in first_run:
+            pair = [B("TS", 15, C, 16), B("HP" if i else "HI", 15, C, 16)]
             tt(B(sb, 16 * i, 16 * i + 16), *(pair[::-1] if m == TEAM - 1 else pair), A.subtract)
         votes(r)
         ship(B(sx), B(lp), "qa%d" % r, False)
@@ -359,44 +380,67 @@ def rank_program(g, core, T, topo):
             name, a = (sb, 0) if k == m and not far else (ld, 128 * far + 32 * k)
             return B(name, a + 16 * kind, a + 16 * kind + 16)
 
-        def sign_of_votes(w):
+        def halves_of_votes(w, spots):
             k = (m - w) % TEAM
             pair = [sums(k, kind, w > m) for kind in (0, 1)]
-            tt(B("AT", 16 * w, 16 * w + 16), *(pair[::-1] if k == TEAM - 1 else pair), A.is_gt)
+            for name, a in spots:
+                a += SCRATCH[name][1][1] // 2 * w
+                tt(B(name, a, a + RUN - NS + 1, NS), *(pair[::-1] if k == TEAM - 1 else pair), A.subtract)
 
-        sign_of_votes(0)
-        for h in range(2):
-            for b in range(4):
-                mm(bank(4 - 4 * h + b), piece("eq", b), piece("es", b), half(lc, h), half(lp, h))
-            for b in range(4):
-                act(B("D", 512 * h + b, 512 * h + 512, 4), bank(4 - 4 * h + b))
+        spots = [("ADD", 0)] + [("MUL", RUN * i + 5) for i in range(4)] + [("MUL", RUN * i) for i in (2, 3)]
+        halves_of_votes(0, spots)
+        ts(B("MORE"), sums(m, 1, False), -0.5 if m == TEAM - 1 else 0.5, None, A.add)
+
+        def spread(made, copied):
+            halves_of_votes(1, [spots[i] for i in made])
+            for i in copied:
+                a = 4 * RUN + spots[i][1]
+                act(B("MUL", a, a + RUN - NS + 1, NS), B("MUL", 4 * RUN + 5, 5 * RUN - 1, NS))
 
         def sub(v, a, n=16):
             a += v[1].start or 0
             return B(v[0], a, a + n)
 
         def places(w):
-            s1, s2, ge, at, po = [B(n, 16 * w, 16 * w + 16) for n in ("S1", "S2", "GE", "AT", "PO")]
-            ti, to, lo, pw, f = B("TI", 160 * w), 192 * w, 96 * w, B("PW", 32 * w), B("FL", 16 * w, 16 * w + 16)
+            po, s1, s2 = B("PO", 16 * w, 16 * w + 16), *[B("ADD", RUN * w + step, RUN * (w + 1), NS) for step in (1, 2)]
+            ti, to, lo, pw, mul, add = B("TI", 10 * RUN * w), 192 * w, 96 * w, B("PW", 32 * w), B("MUL", 4 * RUN * w), B("ADD", RUN * w)
             x = [sums(k, int(k >= (m - w) % TEAM), w > m) for k in range(TEAM)]
-            return [
-                lambda: (tt(s1, x[0], x[1], A.add), tt(s2, x[3], x[2], A.subtract), w and sign_of_votes(1)),
-                lambda: tt(ge, s1, s2, A.is_ge),
-                lambda: tt(f, ge, at, A.is_equal),
-                lambda: (scan(sub(ti, 1, 15), sub(f, 0, 15), B("EVEN", 0, 15), 0.0, A.add, A.mult),
-                         scan(sub(ti, 65, 15), sub(f, 0, 15), B("EVEN", 16, 31), 0.0, A.add, A.mult),
-                         tt(sub(ti, 32), f, B("KAP", 0, 16), A.mult),
-                         tt(sub(ti, 128), f, B("KAP", 16, 32), A.mult)),
-                lambda: tr(B("TO", to, to + 160), sub(ti, 0, 160)),
+            if (m - w) % 2 == 0:
+                x[m] = B("MORE")
+            a, b, c = (0, 2, 1) if m == 2 else (0, 1, 2)
+            both = [(s1, x[a], x[b], A.add), (s2, x[c], x[3], A.subtract)]
+            if m == 1:
+                both.reverse()
+            if m:
+                tt(*both.pop(0))
+
+            def flags(a, b):
+                for i, at, skip in ((0, 1, 0), (1, 4, 0), (2, 0, NS), (3, 2, NS))[a:b]:
+                    scan(sub(ti, 2 * RUN * at + skip, RUN - skip), sub(mul, RUN * i, RUN - skip), sub(add, 0, RUN - skip), 0.0, A.mult, A.add)
+
+            if w > m:
+                head = [lambda: None, lambda: ([tt(*call) for call in both], spread((1, 0, 2), (3, 5, 4, 6))),
+                        lambda: flags(0, 2), lambda: flags(2, 4)]
+            else:
+                head = [lambda: ([tt(*call) for call in both], w and spread((1, 0, 2, 3, 5), (4, 6))), lambda: flags(0, 4)]
+            return head + [
+                lambda: tr(B("TO", to, to + 160), B("TI", 10 * RUN * w + NS - 1, 10 * RUN * (w + 1), NS)),
                 lambda: (scan(B("LO", lo + 1, lo + 48), B("TO", to + 97, to + 144), B("TO", to, to + 47), init, A.add, A.subtract),
                          scan(B("LO", lo + 94, lo + 47, -1), B("TO", to + 190, to + 143, -1), B("TO", to + 95, to + 48, -1),
                               init, A.add, A.subtract)),
                 lambda: tr(sub(pw, 0, 32), B("LO", lo + 32, lo + 64)),
-                lambda: ts(po, sub(pw, 0), q_, None, A.add)]
+                lambda: ts(po, sub(pw, 0), 0.5, q_, A.mult, A.add)]
 
-        for mine, theirs in zip(places(0), places(1)):
-            mine()
-            theirs()
+        mine, theirs = places(0), places(1)
+        for step in mine:
+            step()
+            theirs.pop(0)()
+
+        for h in range(2):
+            for b in range(4):
+                mm(bank(4 - 4 * h + b), piece("eq", b), piece("es", b), half(lc, h), half(lp, h))
+            for b in range(4):
+                act(B("D", 512 * h + b, 512 * h + 512, 4), bank(4 - 4 * h + b))
 
         def source(a, b):
             return ("D", B("OFP", a // 4, b // 4)) if a < K else ("X", B("OFO", (a - K) // 4, (b - K) // 4))
@@ -431,14 +475,20 @@ def rank_program(g, core, T, topo):
                 mm(bank(4 * h + b), piece("wq", b), piece("wp", b), half("zq", h), half("zs", h))
 
         scatter("NO", 0, 16)
-        scatter("NP", 16, 20)
+        early = 0 if theirs else 4
+        if theirs:
+            theirs.pop(0)()
+        else:
+            scatter("NP", 16, 16 + early)
         hold("DO", "NO", 0, C - K)
+        if theirs:
+            theirs.pop(0)()
         offsets("OFO", "DO")
         minus_half(H + K, C)
         minus_half(H, H + K)
         if r == R - 1:
             dma("g", T.od[:], T.NO[0:128:16, :], [B("NO")], [])
-        scatter("NP", 20, 32)
+        scatter("NP", 16 + early, 32)
         minus_half(K, H, "v")
         hold("DP", "NP", C - K, C)
         zpart(K, H)
@@ -473,11 +523,11 @@ def rank_program(g, core, T, topo):
                 dma("y", T.oc[:, 512 * h:512 * h + 512], ap(half("qx%d" % R, h)).bitcast(dt.uint8), [half("qx%d" % R, h)], [])
 
     sx = "sx%d" % R
-    for k in range(4):
-        dma("s", T.osc[4 * k:4 * k + 4, :], T[sx][32 * k:32 * k + 4, :], [B(sx)], [])
     for h in range(2):
         cp(half("YS", h), bank(h))
         dma("y" if h else "s", T.y[:, H * h:H * h + H], ap(half("YS", h)), [half("YS", h)], [])
+    for k in range(4):
+        dma("s", T.osc[4 * k:4 * k + 4, :], T[sx][32 * k:32 * k + 4, :], [B(sx)], [])
     moves = [c for c, call in enumerate(calls) if call[4] in ("soft", "hard")]
     op("g", lambda: g.wait_ge(T.sem.sent, sent[0]), [], [], "c", moves)
     issue()

from concourse.bass import DstId, RemoteDMATransfer
from concourse.mybir import dt, AluOpType, ActivationFunctionType

C, K, R, TEAM = 256, 96, 3, 4
H = C // 2
NS = 7
RUN = 16 * NS
ROUND = 49152.0
FP8, U8, BF, F32, I32, U16 = "float8_e4m3fn_x4", "uint8", "bfloat16", "float32", "int32", "uint16"


def _s(n, d):
    return ("sbuf", [128, n], d)


SCRATCH = {
    "X": _s(1024, BF), "X32": _s(1024, BF), "Z": _s(1024, BF), "Z32": _s(1024, BF), "HB": _s(1024, BF), "D": _s(1024, BF),
    "U": _s(512, BF), "Vv": _s(512, BF), "uq": _s(128, FP8), "us": _s(128, U8), "up": _s(256, FP8), "ups": _s(256, U8),
    "vq": _s(128, FP8), "vs": _s(128, U8), "wq": _s(512, FP8), "wp": _s(512, U8), "zq": _s(256, FP8), "zs": _s(256, U8),
    "ET": _s(520, BF), "eq": _s(512, FP8), "es": _s(512, U8),
    "pi": _s(8, I32), "uo": _s(16, I32), "uo16": _s(16, U16), "IO": _s(256, BF), "I16": _s(128, BF),
    "PP": _s(24, F32), "TMP": _s(16, F32), "NE": _s(128, BF),
    "HALF": _s(256, BF), "FROM": _s(128, BF), "PAST": _s(128, BF),
    "CD4": _s(160, BF), "MUL": _s(8 * RUN, BF), "ADD": _s(2 * RUN, "float16"), "STEP": _s(128, BF), "IR": _s(256, BF),
    "SBs": _s(256, F32), "AI": _s(256, BF), "TS": _s(256, BF), "HP": _s(256, BF), "HI": _s(256, BF),
    "MORE": _s(16, BF), "TI": _s(20 * RUN, BF), "TO": _s(384, BF), "LO": _s(192, BF),
    "ONE": _s(256, BF), "PW": _s(64, BF), "PO": _s(32, U16),
    "NO": _s(256, BF), "NP": _s(256, BF), "DO": _s(160, BF), "DP": _s(96, BF), "OFO": _s(40, U16), "OFP": _s(24, U16),
    "YS": _s(256, F32),
    "ps": ("psum", [128, 4096], F32),
}
for _r in range(R + 1):
    SCRATCH["qx%d" % _r] = _s(256, FP8)
    SCRATCH["sx%d" % _r] = _s(256, U8)
for _r in range(R):
    SCRATCH["lc%d" % _r] = _s(256, FP8)
    SCRATCH["lp%d" % _r] = _s(256, U8)
    SCRATCH["sb%d" % _r] = _s(32, BF)
    SCRATCH["ld%d" % _r] = _s(256, BF)
SHARED = ["k%d" % i for i in range(120)]
ONCE = ["d%d" % i for i in range(16)]
SEMAPHORES = SHARED + ONCE + ["sent"]
SEMAPHORES += ["%s%d" % (n, r) for n in ("va", "vb", "qa", "qb") for r in range(R)]

A = AluOpType
COPY = ActivationFunctionType.Copy


def rank_program(g, core, T, topo):
    rank = T.rank_of(core)
    if rank is None:
        return
    N = len(T.cores)
    m, team = rank % TEAM, rank // TEAM
    eng = {"v": g.vector, "s": g.scalar, "t": g.tensor, "g": g, "y": g.sync}
    know = {q: set() for q in eng}
    calls, log = [], {}

    def cols(v):
        w = SCRATCH[v[0]][1][1]
        r = range(*v[1].indices(w))
        if SCRATCH[v[0]][0] == "psum":
            return set(c // 512 for c in (r[0], r[-1]))
        return set(r)

    def B(name, a=None, b=None, s=None):
        return (name, slice(a, b, s))

    def bank(i):
        return B("ps", 512 * i, 512 * i + H)

    def ap(v):
        return T[v[0]][:, v[1]]

    def order(q, reads, writes, more):
        need = set(more)
        for v, wr in [(v, False) for v in reads] + [(v, True) for v in writes]:
            cs = cols(v)
            ps = SCRATCH[v[0]][0] == "psum"
            for t, c2, w2 in log.get(v[0], []):
                if (wr or w2 or (ps and calls[t][0] != q)) and cs & c2:
                    need.add(t)
        waits = []
        for t in sorted(need, reverse=True):
            if t not in know[q]:
                waits.append(t)
                know[q] |= calls[t][3] | {t}
        return waits

    def op(q, fn, reads, writes, kind="c", more=()):
        waits = order(q, reads, writes, more) if q in know else []
        calls.append((q, fn, waits, set(know.get(q, ())), kind))
        for v, wr in [(v, False) for v in reads] + [(v, True) for v in writes]:
            log.setdefault(v[0], []).append((len(calls) - 1, cols(v), wr))
        return len(calls) - 1

    def arrival(sem, val, writes):
        return op("far", (sem, val), [], writes, "far")

    def issue():
        by = {t: set() for t in range(len(calls))}
        for c, call in enumerate(calls):
            for t in call[2]:
                by[t].add(c)
        lot = {t: [t] for t in by}

        def free(c, t, both):
            return t in calls[c][3] or any(u > t and calls[u][0] == calls[t][0] and calls[t][4] == "c" and c in by[u] for u in both)

        for call in calls:
            for i, t in enumerate(call[2]):
                for u in call[2][:i]:
                    both = lot[t] + lot[u]
                    if lot[t] is not lot[u] and calls[t][4] == calls[u][4] != "far" and all(
                            free(c, x, both) for y in both for c in by[y] for x in both):
                        for x in both:
                            lot[x] = both
        done, seen = {q: set() for q in eng}, []
        for c, (q, fn, waits, _, kind) in enumerate(calls):
            for t in list(waits):
                if t in done[q]:
                    waits.remove(t)
                for x in lot[t]:
                    done[q] |= seen[x] | {x}
            seen.append(set(done.get(q, ())))
        sem_of, held, once = {}, [(n, 0, []) for n in SHARED], list(ONCE)
        for c, (q, fn, waits, _, kind) in enumerate(calls):
            mine = lot[c]
            if kind == "far":
                sem_of[c] = fn
                continue
            if c not in sem_of and any(by[x] for x in mine):
                if kind == "c":
                    i = min(i for i, h in enumerate(held) if all(y in seen[x] for y in h[2] for x in mine))
                    n, val, _ = held.pop(i)
                    val += len(mine)
                    held.append((n, val, mine))
                else:
                    n, val = once.pop(), 16 * len(mine)
                for x in mine:
                    sem_of[x] = (n, val)
            for t in waits:
                eng[q].wait_ge(T.sem[sem_of[t][0]], sem_of[t][1])
            made = fn()
            if c in sem_of:
                made.then_inc(T.sem[sem_of[c][0]], 1 if kind == "c" else 16)

    V, S = g.vector, g.scalar

    def tt(o, a, b, alu):
        return op("v", lambda: V.tensor_tensor(ap(o), ap(a), ap(b), alu), [a, b], [o])

    def ts(o, a, s1, s2, op0, op1=None):
        rd = [a] + [s for s in (s1, s2) if isinstance(s, tuple)]
        a1, a2 = [ap(s) if isinstance(s, tuple) else s for s in (s1, s2)]
        if op1 is None:
            return op("v", lambda: V.tensor_scalar(ap(o), ap(a), a1, None, op0), rd, [o])
        return op("v", lambda: V.tensor_scalar(ap(o), ap(a), a1, a2, op0, op1), rd, [o])

    def cp(o, a):
        return op("v", lambda: V.tensor_copy(ap(o), ap(a)), [a], [o])

    def fill(o, c):
        return op("v", lambda: V.memset(ap(o), c), [], [o])

    def scan(o, d0, d1, init, op0, op1):
        rd = [d0, d1] + ([init] if isinstance(init, tuple) else [])
        i = ap(init) if isinstance(init, tuple) else init
        return op("v", lambda: V.tensor_tensor_scan(ap(o), ap(d0), ap(d1), i, op0, op1), rd, [o])

    def tr(o, a):
        return op("v", lambda: V.transpose(ap(o), ap(a)), [a], [o])

    def quant(c, s, a):
        return op("v", lambda: V.quantize_mx(ap(c), ap(s), ap(a)), [a], [c, s])

    def act(o, a, scale=1.0):
        return op("s", lambda: S.activation(ap(o), ap(a), COPY, scale=scale), [a], [o])

    def lin(o, a, scale, bias):
        rd = [a] + [s for s in (scale, bias) if isinstance(s, tuple)]
        a1, a2 = [ap(s) if isinstance(s, tuple) else s for s in (scale, bias)]
        return op("s", lambda: S.activation(ap(o), ap(a), ActivationFunctionType.Identity, bias=a2, scale=a1), rd, [o])

    def mm(o, lc, ls, rc, rs):
        return op("t", lambda: g.tensor.matmul_mx(ap(o), ap(lc), ap(ls), ap(rc), ap(rs), True, True), [lc, ls, rc, rs], [o])

    def dma(q, o, i, reads, writes, more=()):
        return op(q, lambda: eng[q].dma_start(o, i), reads, writes, "soft" if q == "g" else "hard", more)

    def iota(o, pattern, step=0):
        small = SCRATCH[o[0]][2] != I32
        return op("g", lambda: g.iota(ap(o), pattern, 0, step, allow_small_or_imprecise_dtypes=small), [], [o])

    def half(name, h, k=1):
        return B(name, k * H * h, k * H * (h + 1))

    def piece(name, b):
        return B(name, 128 * b, 128 * b + 128)

    def bits(engines):
        return sum(1 << e for e in engines)

    sent = [0]
    nxt, prev = T.cores[(rank + 1) % N], (rank - 1) % N

    def ship(src, dst, sem, codes):
        rid, pid = topo.addr(nxt, core)
        a, b = (ap(src).bitcast(dt.uint8), ap(dst).bitcast(dt.uint8)) if codes else (ap(src), ap(dst))
        op("g", lambda: g.remote_dma(b, a, T.sem[sem], T.sem.sent, pid, rid, topo.mask(core, nxt)), [src], [])
        sent[0] += len(topo.engines(core, nxt))

    def single(k):
        return k + 1 if k + 1 < TEAM else k - 1

    first_run = (0, 1) if m < 2 else (1, 0)

    def votes(r):
        sb, ld = "sb%d" % r, "ld%d" % r

        def run(to, kinds, base, sem, share, i):
            rid, pid = topo.addr(T.cores[to], core)
            es = topo.engines(core, T.cores[to])
            n = len(es) // share
            a, b = 16 * kinds[0], 16 * kinds[-1] + 16
            sent[0] += n
            return (RemoteDMATransfer(dst_ids=[DstId(rid=rid, pnc=pid)], dma_engine_mask=bits(es[n * i:n * i + n]),
                                      remote_sem=T.sem[sem], src=ap(B(sb, a, b)), dst=ap(B(ld, base + a, base + b))), B(sb, a, b))

        def mate(j, share, i):
            return run(team * TEAM + j, (0, 1) if j == m + 1 else (int(j < m),), 32 * m, ("vb%d" if share == 1 else "va%d") % r, share, i)

        two = [mate(j, 2, i) for i, j in enumerate(j for j in range(TEAM) if j not in (m, single(m)))]
        far = run(((team + 1) * TEAM) % N, (0, 1) if m == TEAM - 1 else (0,), 128 + 32 * m, "vb%d" % r, 1, 0)
        for part in (two, [mate(single(m), 1, 0)], [far]):
            op("g", lambda part=part: g.remote_dma_fused([t for t, _ in part], local_sem=T.sem.sent), [v for _, v in part], [])

    def inflow(src, share):
        return len(topo.engines(T.cores[src], core)) // share

    p_, row, u_, t_, odd, sign, top, q_, low, init, u1, ufix, oadd, jump, first = [B("PP", i, i + 1) for i in range(15)]

    dma("y", T.X[:, 0:512], T.x[:, 0:512], [], [half("X", 0, 4)])
    dma("y", T.U[:], T.u[:], [], [B("U")])
    dma("y", T.X[:, 512:1024], T.x[:, 512:1024], [], [half("X", 1, 4)])
    iota(B("pi", 0, 1), [[0, 1]], 1)
    iota(B("uo"), [[1, 2], [16, 8]])
    iota(B("I16"), [[0, 8], [1, 16]])
    fill(B("ONE"), 1.0)
    fill(B("ET"), 0.0)
    ts(B("pi", 1, 2), B("pi", 0, 1), 15, None, A.bitwise_and)
    ts(B("pi", 2, 3), B("pi", 0, 1), 2, 3, A.arith_shift_right, A.bitwise_and)
    ts(B("pi", 3, 4), B("pi", 0, 1), 3, None, A.bitwise_and)
    ts(B("pi", 4, 5), B("pi", 0, 1), 4, 1, A.arith_shift_right, A.bitwise_and)
    cp(B("uo16"), B("uo"))
    cp(B("PP", 0, 5), B("pi", 0, 5))
    lin(sign, odd, -2.0, 1.0)
    lin(top, odd, 15.0, 0.0)
    lin(u1, u_, 1.0, 1.0)
    lin(q_, row, sign, top)

    def deciding_columns(k):
        off = B("uo16", 8 * k, 8 * k + 8)
        op("s", lambda: S.activation(ap(piece("ups", k)), T.us[:].indirect(ap(off)), COPY), [B("us"), off], [piece("ups", k)])
        op("v", lambda: V.tensor_copy(ap(piece("up", k)).bitcast(dt.uint32), T.uq[:].bitcast(dt.uint32).indirect(ap(off))),
           [B("uq"), off], [piece("up", k)])

    def constants_of_the_orders():
        ts(B("ET", 3, 515, 4), B("IO", 0, 128), p_, None, A.is_equal)
        ts(ufix, u_, 3.0, 1024.0, A.is_lt, A.mult)
        ts(B("TMP", 0, 4), B("IO", 0, 4), u_, 1024.0, A.is_equal, A.mult)
        ts(B("TMP", 4, 8), B("IO", 0, 4), u1, -256.0, A.is_equal, A.mult)
        ts(B("FROM"), B("NE"), low, None, A.add)
        ts(B("PAST"), B("NE"), low, 0.5, A.add, A.add)

    def constants_of_the_unpacking():
        tt(B("TMP", 8, 12), B("TMP", 0, 4), B("TMP", 4, 8), A.add)
        lin(B("STEP"), half("ONE", 0), sign, 0.0)
        lin(jump, odd, 30.0, 1.0)
        lin(first, odd, -15.0, -1.0)
        lin(init, row, 32.0, 0.0)
        for i in range(2):
            lin(B("PP", 16 + i, 17 + i), q_, -1024.0, 1024.0 * (C - i))
            lin(B("PP", 18 + i, 19 + i), odd, 1024.0 * (2 * i - 1), 1024.0 * (1 - i))
        for step, c in enumerate((0.0, 1024.0, 1.0, 2.0 ** -18, 1.0)):
            act(B("MUL", step, None, NS), B("ONE", 0, 128), c)
        lin(B("STEP", 0, H, 16), B("ONE", 0, 8), jump, 0.0)
        for step, c in ((3, ROUND), (4, -ROUND), (5, 0.0), (6, 0.0)):
            ts(B("ADD", step, None, NS), B("ONE", 0, 32), c, None, A.mult)
        for w in range(2):
            last = [B("MUL", RUN * (4 * w + i) + NS - 1, RUN * (4 * w + i + 1), NS) for i in range(4)]
            for i in range(2):
                lin(last[i], B("IO", 0, 16), -16384.0, B("PP", 16 + i, 17 + i))
                lin(last[2 + i], B("ONE", 0, 16), B("PP", 18 + i, 19 + i), 0.0)
            act(B("TI", 10 * RUN * w + NS - 1, 10 * RUN * (w + 1), NS), B("ONE", 0, 160), 0.0)
            act(B("TO", 192 * w + 160, 192 * w + 192), B("ONE", 0, 32), 0.0)
        lin(oadd, t_, 1.0, ufix)
        for k in range(4):
            lin(B("CD4", k, None, 4), B("ONE", 0, 40), B("TMP", 8 + k, 9 + k), 0.0)
        for b in range(4):
            quant(piece("eq", b), piece("es", b), B("ET", 3 - b, 515 - b))
            if b % 2:
                scan(half("IR", b // 2), B("STEP"), half("ONE", 0), B("IR", H - 1, H) if b // 2 else first, A.add, A.mult)

    def quantise_state(r, h):
        qx, sx = "qx%d" % r, "sx%d" % r
        quant(half(qx, h), half(sx, h), half("X", h, 4))
        if r < R and h == 0:
            ship(half(qx, 0), half("lc%d" % r, 0), "qa%d" % r, True)

    def score(r, h, k):
        mm(bank(2 * h + 1 - k), piece("up", k), piece("ups", k), half("qx%d" % r, h), half("sx%d" % r, h))

    quantise_state(0, 0)
    scan(B("IO"), B("ONE"), B("ONE"), -1.0, A.add, A.mult)
    quant(B("uq"), B("us"), B("U"))
    fill(B("HALF"), -0.5)
    deciding_columns(1)
    quantise_state(0, 1)
    deciding_columns(0)
    ts(B("NE"), B("I16"), q_, 1024.0, A.not_equal, A.mult)
    lin(low, q_, 0.5, -8.0)
    for k in (1, 0):
        for h in range(2):
            score(0, h, k)
    constants_of_the_orders()

    for r in range(R):
        qx, sx, lc, lp, sb, ld = ["%s%d" % (n, r) for n in ("qx", "sx", "lc", "lp", "sb", "ld")]
        arrival("qa%d" % r, 2 * inflow(prev, 1), [B(lp), half(lc, 0)])
        arrival("qb%d" % r, inflow(prev, 1), [half(lc, 1)])
        soon, late = [[k for k in range(TEAM) if k != m and (single(k) == m) == alone] for alone in (False, True)]
        came = arrival("va%d" % r, sum(inflow(team * TEAM + k, 2) for k in soon), [B(ld, 32 * k, 32 * k + 32) for k in soon])
        if m:
            arrival("vb%d" % r, sum(inflow(team * TEAM + k, 1) for k in late), [B(ld, 32 * k, 32 * k + 32) for k in late])
        else:
            arrival("vb%d" % r, sum(inflow(prev - i, 1) for i in range(TEAM)), [B(ld, 128, 256)])

        def vote(h):
            n = H // 2
            for a in range(0, H, n):
                act(B("SBs", H * h + a, H * h + a + n), B("ps", 1024 * h + a, 1024 * h + a + n))
            for a in range(0, H, n):
                tt(B("AI", H * h + a, H * h + a + n), B("ps", 1024 * h + 512 + a, 1024 * h + 512 + a + n), B("SBs", H * h + a, H * h + a + n), A.is_ge)

        def whole(a, b):
            scan(B("TS", a, b), B("AI", a, b), B("HALF", a, b), B("TS", a - 1, a) if a else 0.0, A.add, A.add)

        def tails(a, b):
            for kind in first_run:
                if kind:
                    scan(B("HP", a, b), B("FROM", 0, b - a), B("AI", a, b), 0.0, A.min, A.add)
                else:
                    scan(B("HI", a, b), B("AI", a, b), B("PAST", 0, b - a), 0.0, A.add, A.min)

        vote(0)
        if r:
            whole(0, H)
        vote(1)
        tails(0, H)
        whole(H if r else 0, C)
        tails(H, C)
        for i in first_run:
            pair = [B("TS", 15, C, 16), B("HP" if i else "HI", 15, C, 16)]
            tt(B(sb, 16 * i, 16 * i + 16), *(pair[::-1] if m == TEAM - 1 else pair), A.subtract)
        votes(r)
        ship(B(sx), B(lp), "qa%d" % r, False)
        ship(half(qx, 1), half(lc, 1), "qb%d" % r, True)

        if r == 0:
            constants_of_the_unpacking()
            dma("y", T.wq[:].bitcast(dt.uint8), T.wc[:], [], [B("wq")], [came])
            dma("y", T.wp[:], T.ws[:], [], [B("wp")])
        if r == 1:
            dma("y", T.Vv[:], T.v[:], [B("X", 0, 4)], [B("Vv")])
        if r == R - 1:
            quant(B("vq"), B("vs"), B("Vv"))

        def sums(k, kind, far):
            name, a = (sb, 0) if k == m and not far else (ld, 128 * far + 32 * k)
            return B(name, a + 16 * kind, a + 16 * kind + 16)

        def halves_of_votes(w, spots):
            k = (m - w) % TEAM
            pair = [sums(k, kind, w > m) for kind in (0, 1)]
            for name, a in spots:
                a += SCRATCH[name][1][1] // 2 * w
                tt(B(name, a, a + RUN - NS + 1, NS), *(pair[::-1] if k == TEAM - 1 else pair), A.subtract)

        spots = [("ADD", 0)] + [("MUL", RUN * i + 5) for i in range(4)] + [("MUL", RUN * i) for i in (2, 3)]
        halves_of_votes(0, spots)
        ts(B("MORE"), sums(m, 1, False), -0.5 if m == TEAM - 1 else 0.5, None, A.add)

        def spread(made, copied):
            halves_of_votes(1, [spots[i] for i in made])
            for i in copied:
                a = 4 * RUN + spots[i][1]
                act(B("MUL", a, a + RUN - NS + 1, NS), B("MUL", 4 * RUN + 5, 5 * RUN - 1, NS))

        def sub(v, a, n=16):
            a += v[1].start or 0
            return B(v[0], a, a + n)

        def places(w):
            po, s1, s2 = B("PO", 16 * w, 16 * w + 16), *[B("ADD", RUN * w + step, RUN * (w + 1), NS) for step in (1, 2)]
            ti, to, lo, pw, mul, add = B("TI", 10 * RUN * w), 192 * w, 96 * w, B("PW", 32 * w), B("MUL", 4 * RUN * w), B("ADD", RUN * w)
            x = [sums(k, int(k >= (m - w) % TEAM), w > m) for k in range(TEAM)]
            if (m - w) % 2 == 0:
                x[m] = B("MORE")
            a, b, c = (0, 2, 1) if m == 2 else (0, 1, 2)
            both = [(s1, x[a], x[b], A.add), (s2, x[c], x[3], A.subtract)]
            if m == 1:
                both.reverse()
            if m:
                tt(*both.pop(0))

            def flags(a, b):
                for i, at, skip in ((0, 1, 0), (1, 4, 0), (2, 0, NS), (3, 2, NS))[a:b]:
                    scan(sub(ti, 2 * RUN * at + skip, RUN - skip), sub(mul, RUN * i, RUN - skip), sub(add, 0, RUN - skip), 0.0, A.mult, A.add)

            if w > m:
                head = [lambda: None, lambda: ([tt(*call) for call in both], spread((1, 0, 2), (3, 5, 4, 6))),
                        lambda: flags(0, 2), lambda: flags(2, 4)]
            else:
                head = [lambda: ([tt(*call) for call in both], w and spread((1, 0, 2, 3, 5), (4, 6))), lambda: flags(0, 4)]
            return head + [
                lambda: tr(B("TO", to, to + 160), B("TI", 10 * RUN * w + NS - 1, 10 * RUN * (w + 1), NS)),
                lambda: (scan(B("LO", lo + 1, lo + 48), B("TO", to + 97, to + 144), B("TO", to, to + 47), init, A.add, A.subtract),
                         scan(B("LO", lo + 94, lo + 47, -1), B("TO", to + 190, to + 143, -1), B("TO", to + 95, to + 48, -1),
                              init, A.add, A.subtract)),
                lambda: tr(sub(pw, 0, 32), B("LO", lo + 32, lo + 64)),
                lambda: ts(po, sub(pw, 0), 0.5, q_, A.mult, A.add)]

        mine, theirs = places(0), places(1)
        for step in mine:
            step()
            theirs.pop(0)()

        for h in range(2):
            for b in range(4):
                mm(bank(4 - 4 * h + b), piece("eq", b), piece("es", b), half(lc, h), half(lp, h))
            for b in range(4):
                act(B("D", 512 * h + b, 512 * h + 512, 4), bank(4 - 4 * h + b))

        def source(a, b):
            return ("D", B("OFP", a // 4, b // 4)) if a < K else ("X", B("OFO", (a - K) // 4, (b - K) // 4))

        def minus_half(a, b, q="s"):
            o, (win, off) = B("HB", 4 * a, 4 * b), source(a, b)
            if q == "s":
                op("s", lambda: S.activation(ap(o), T[win][:].indirect(ap(off)), COPY, scale=-0.5), [B(win), off], [o])
            else:
                op("v", lambda: V.tensor_scalar(ap(o), T[win][:].indirect(ap(off)), -0.5, None, A.mult), [B(win), off], [o])

        def zpart(a, b):
            o, hb, (win, off) = B("Z", 4 * a, 4 * b), B("HB", 4 * ((a + H) % C), 4 * ((a + H) % C + b - a)), source(a, b)
            op("v", lambda: V.tensor_tensor(ap(o), T[win][:].indirect(ap(off)), ap(hb), A.add), [B(win), off, hb], [o])

        def scatter(nn, a, b):
            off, j = B("PO", a, b), B("IR", 16 * (a % 16), 16 * (a % 16 + b - a))
            op("v", lambda: V.tensor_copy(T[nn][:].indirect(ap(off)), ap(j)), [j, off], [B(nn)])

        def hold(dg, nn, a, b):
            scan(B(dg), B("CD4", 0, b - a), B(nn, a, b), 0.0, A.add, A.min)

        def offsets(of, dg):
            ts(B(of), B(dg, 3, None, 4), 4.0, oadd, A.mult, A.add)

        def times32(a, b):
            act(B("Z32", 4 * a, 4 * b), B("Z", 4 * a, 4 * b), 32.0)

        def layer(h):
            quant(half("zq", h), half("zs", h), half("Z", h, 4))
            for b in range(4):
                mm(bank(4 * h + b), piece("wq", b), piece("wp", b), half("zq", h), half("zs", h))

        scatter("NO", 0, 16)
        early = 0 if theirs else 4
        if theirs:
            theirs.pop(0)()
        else:
            scatter("NP", 16, 16 + early)
        hold("DO", "NO", 0, C - K)
        if theirs:
            theirs.pop(0)()
        offsets("OFO", "DO")
        minus_half(H + K, C)
        minus_half(H, H + K)
        if r == R - 1:
            dma("g", T.od[:], T.NO[0:128:16, :], [B("NO")], [])
        scatter("NP", 16 + early, 32)
        minus_half(K, H, "v")
        hold("DP", "NP", C - K, C)
        zpart(K, H)
        offsets("OFP", "DP")
        minus_half(0, K // 2)
        minus_half(K // 2, K)
        zpart(H + K, C)
        zpart(0, K)
        zpart(H, H + K // 2)
        layer(0)
        times32(0, H)
        times32(H + K, C)
        zpart(H + K // 2, H + K)
        times32(H, H + K)
        layer(1)

        for h in range(2):
            for b in range(4):
                rows = (512 * h + b, 512 * h + 512, 4)
                tt(B("X32", *rows), bank(4 * h + b), B("Z32", *rows), A.add)
                if (h, b) != (1, 3):
                    act(B("X", *rows), B("X32", *rows), 0.03125)
        for h in range(2):
            quantise_state(r + 1, h)
            if h == 0:
                ts(B("X", *rows), B("X32", *rows), 0.03125, None, A.mult)
            if r + 1 < R:
                score(r + 1, h, 1)
                score(r + 1, h, 0)
            else:
                mm(bank(h), B("vq"), B("vs"), half("qx%d" % R, h), half("sx%d" % R, h))
                dma("y", T.oc[:, 512 * h:512 * h + 512], ap(half("qx%d" % R, h)).bitcast(dt.uint8), [half("qx%d" % R, h)], [])

    sx = "sx%d" % R
    for h in range(2):
        cp(half("YS", h), bank(h))
        dma("y" if h else "s", T.y[:, H * h:H * h + H], ap(half("YS", h)), [half("YS", h)], [])
    for k in range(4):
        dma("s", T.osc[4 * k:4 * k + 4, :], T[sx][32 * k:32 * k + 4, :], [B(sx)], [])
    moves = [c for c, call in enumerate(calls) if call[4] in ("soft", "hard")]
    op("g", lambda: g.wait_ge(T.sem.sent, sent[0]), [], [], "c", moves)
    issue()
